import numpy as np
import ml_dtypes


def mxq(x, axis, fmt="e4m3"):
    dtype, down = {"e4m3": (ml_dtypes.float8_e4m3fn, 7), "e5m2": (ml_dtypes.float8_e5m2, 14)}[fmt]
    v = np.moveaxis(np.asarray(x, np.float32).astype(ml_dtypes.bfloat16).astype(np.float64), axis, -1)
    blocks = v.reshape(v.shape[:-1] + (-1, 32))
    amax = np.abs(blocks).max(-1, keepdims=True)
    byte = np.maximum(np.where(amax > 0, np.frexp(amax)[1] - 1 + 127, 0) - down, 1)
    scale = np.exp2(byte - 127.0)
    codes = (blocks / scale).astype(np.float32).astype(dtype).astype(np.float64)
    return np.moveaxis((codes * scale).reshape(v.shape), -1, axis)


WIDE = False


def mx_kscale(k):
    if not WIDE:
        return np.ones(k)
    levels = np.array([10, -10, 5, -5, 0])
    if k % 512:
        return np.exp2(np.random.permutation(np.resize(levels, k // 32))).repeat(32)
    a = np.empty((k // 512, 16))
    for p in range(k // 512):
        a[p, :8] = np.random.permutation(np.resize(levels, 8))
        for g in range(8):
            far = levels[np.abs(levels - a[p, g]) >= 10]
            a[p, g + 8] = far[np.random.randint(len(far))]
    return np.exp2(a.ravel()).repeat(32)


def f64(x):
    return np.asarray(x).astype(np.float64)


def striped(idx):
    return np.tile(idx.reshape(-1, 16).T, (8, 1)).astype(np.uint16)


def unstriped(offs):
    return offs[:16].T.reshape(-1).astype(np.int64)


E2M1 = np.array([0.0, 0.5, 1.0, 1.5, 2.0, 3.0, 4.0, 6.0, -0.0, -0.5, -1.0, -1.5, -2.0, -3.0, -4.0, -6.0])


def pack_weight(w, fmt):
    k, n = w.shape
    w = f64(np.asarray(w, np.float32).astype(ml_dtypes.bfloat16)).reshape(k // 32, 32, n)
    amax = np.abs(w).max(1)
    if fmt == "e4m3":
        byte = np.frexp(amax)[1] - 1 + 127 - 7
    else:
        mant, ex = np.frexp(amax / 6.0)
        byte = np.where(mant > 0.5, ex, ex - 1) + 127
    byte = np.clip(np.where(amax > 0, byte, 1), 1, 254)
    scaled = (w * np.exp2(127.0 - byte)[:, None, :]).reshape(k, n).astype(np.float32)
    by_word = np.ascontiguousarray(scaled.reshape(k // 512, 128, 4, n).transpose(0, 1, 3, 2))
    if fmt == "e4m3":
        words = by_word.astype(ml_dtypes.float8_e4m3fn).view(np.uint8)
    else:
        c = by_word.astype(ml_dtypes.float4_e2m1fn).view(np.uint8) & 0xF
        words = (c[..., 0::2] | (c[..., 1::2] << 4)).reshape(k // 512, 128, 2 * n)
    return np.ascontiguousarray(words), np.ascontiguousarray(byte.astype(np.uint8).reshape(k // 512, 16, n))


def unpack_weight(words, scales, fmt):
    g, _, n = scales.shape
    words = np.ascontiguousarray(words).reshape(g, 128, n, -1)
    if fmt == "e4m3":
        vals = words.view(ml_dtypes.float8_e4m3fn).astype(np.float64)
    else:
        nib = np.empty((g, 128, n, 4), np.uint8)
        nib[..., 0::2] = words & 0xF
        nib[..., 1::2] = words >> 4
        vals = E2M1[nib]
    vals = vals * np.repeat(np.exp2(scales.astype(np.float64) - 127.0), 8, axis=1)[..., None]
    return vals.transpose(0, 1, 3, 2).reshape(g * 512, n)


def gelu(v):
    return 0.5 * v * (1.0 + np.tanh(np.sqrt(2.0 / np.pi) * (v + 0.044715 * v**3)))


K, T, S, H, T2, T3, S2, P = 1024, 2048, 1024, 512, 2048, 2048, 512, 1024

def setup_inputs():
    n = np.random.standard_normal
    s = mx_kscale(K)[:, None]
    u = mx_kscale(H)[:, None]
    tab_words, tab_scales = pack_weight(n((K, T)) * s, "e4m3")
    tab2_words, tab2_scales = pack_weight(n((H, T3)) / np.sqrt(H) / u, "e4m3")
    w1_words, w1_scales = pack_weight(n((K, H)) / np.sqrt(K) / s, "e2m1")
    w3_words, w3_scales = pack_weight(n((K, H)) / np.sqrt(K) / s * u.T, "e4m3")
    return {
        "tab_words": tab_words, "tab_scales": tab_scales,
        "tab2_words": tab2_words, "tab2_scales": tab2_scales,
        "w1_words": w1_words, "w1_scales": w1_scales,
        "w2": (n((K, H)) / np.sqrt(K) / s).astype(np.float32),
        "w3_words": w3_words, "w3_scales": w3_scales,
        "page0": (n((H, T2)) * u).astype(np.float32),
        "wgs": np.exp(0.3 * n((128, S))).astype(np.float32),
        "avail": np.exp(0.3 * n(S2)).astype(np.float32),
        "offs": striped(np.random.permutation(T)[:S]),
        "offs2": striped(np.random.permutation(T3)[:S2]),
        "offs3": striped(np.random.permutation(T2)[:S]),
        "offs4": striped(np.random.permutation(T2)[:P]),
    }

def reference(tab_words, tab_scales, tab2_words, tab2_scales, w1_words, w1_scales, w2,
              w3_words, w3_scales, page0, wgs, avail, offs, offs2, offs3, offs4):
    v = unpack_weight(tab_words, tab_scales, "e4m3")[:, unstriped(offs)]
    v2 = unpack_weight(tab2_words, tab2_scales, "e4m3")[:, unstriped(offs2)]
    a = unpack_weight(w1_words, w1_scales, "e2m1").T @ v
    b = mxq(f64(w2), 0, "e4m3").T @ v
    c = unpack_weight(w3_words, w3_scales, "e4m3").T @ v
    h = np.minimum(a, b) * c
    page = f64(page0).copy()
    page[:, unstriped(offs3)] = np.tile(f64(wgs), (H // 128, 1)) * h
    e = v2.T @ mxq(page, 0, "e4m3")
    x = e[:, unstriped(offs4)]
    return f64(avail)[:, None] / (1.0 + np.square(x))

@@ -1,0 +1,257 @@
+from contextlib import ExitStack
+
+import concourse.mybir as mybir
+
+K, T, S, H, T2, T3, S2, PK = 1024, 2048, 1024, 512, 2048, 2048, 512, 1024
+FLOPS = 2 * (3 * K * H * S + H * S2 * T2)
+
+F32 = mybir.dt.float32
+BF16 = mybir.dt.bfloat16
+I32 = mybir.dt.int32
+U32 = mybir.dt.uint32
+U16 = mybir.dt.uint16
+U8 = mybir.dt.uint8
+FP8X4 = mybir.dt.float8_e4m3fn_x4
+FP4X4 = mybir.dt.float4_e2m1fn_x4
+ALU = mybir.AluOpType
+ACT = mybir.ActivationFunctionType
+
+P = 128
+N = 512
+
+
+def tile_list_tow_dispatch_scores_kernel(
+    tc, tab_words, tab_scales, tab2_words, tab2_scales, w1_words, w1_scales, w2,
+    w3_words, w3_scales, page0, wgs, avail, offs, offs2, offs3, offs4, out,
+):
+    nc = tc.nc
+    with ExitStack() as ctx:
+        keep = ctx.enter_context(tc.tile_pool(name="keep", bufs=1))
+        ring = ctx.enter_context(tc.tile_pool(name="ring", bufs=8))
+        psum = ctx.enter_context(tc.psum_pool(name="psum", bufs=1))
+        banks = {"a": 4, "b": 2, "c": 2}
+
+        def bank(tag):
+            return psum.tile([P, N], F32, name="acc_" + tag, tag=tag, bufs=banks[tag])
+
+        def held(name, shape, dtype):
+            return keep.tile(shape, dtype, name=name, align_bytes=64)
+
+        list1 = held("list1", [P, S // 16], U16)
+        list2 = held("list2", [P, S2 // 16], U16)
+        list3 = held("list3", [P, S // 16], U16)
+        list4 = held("list4", [P, PK // 16], U16)
+
+        tab_s = held("tab_s", [P, T], U8)
+        v_s1 = held("v_s1", [P, S], U8)
+        w_s_raw = held("w_s_raw", [P, 2 * H], U8)
+        tab2_s = held("tab2_s", [P, T3], U8)
+        for plane in (tab_s, w_s_raw, v_s1, tab2_s):
+            nc.vector.memset(plane[:].bitcast(I32), 0)
+
+        tab_w = [held("tab_w%d" % a, [P, T], I32) for a in range(2)]
+        w1_raw = held("w1_raw", [P, 2 * H // 2], I32)
+        avail_sb = held("avail_sb", [P, 4], F32)
+        w_s_rows = w_s_raw[:].bitcast(I32).rearrange("p (a y) -> p a y", a=2)
+        w2_raw = [held("w2_raw%d" % a, [P, 4, H], F32) for a in range(2)]
+        w3_raw = held("w3_raw", [P, 2 * H], I32)
+        wgs_rows = wgs.rearrange("(m t) j -> m t j", t=4)
+        page_rows = page0.rearrange("(p t) c -> p t c", t=4)
+        gain = [held("gain%d" % t, [P, S], F32) for t in range(4)]
+        page = [held("page%d" % t, [P, T2], F32) for t in range(4)]
+        tab2_w = held("tab2_w", [P, T3], I32)
+
+        def load_words(tile, words):
+            nc.sync.dma_start(tile[:], words.rearrange("p t i -> p (t i)").bitcast(I32))
+
+        def load_w2(a):
+            nc.sync.dma_start(w2_raw[a][:], w2[512 * a : 512 * (a + 1), :].rearrange("(p j) y -> p j y", j=4))
+
+        def load_scales(rows, scales, first):
+            for q in range(4):
+                nc.sync.dma_start(rows[32 * q + first : 32 * q + first + 4], scales[:, 4 * q : 4 * q + 4, :].rearrange("a q y -> q a y").bitcast(I32))
+
+        def load_tab_scales():
+            for q in range(4):
+                nc.sync.dma_start(tab_s[32 * q : 32 * q + 8, :].bitcast(I32), tab_scales[:, 4 * q : 4 * q + 4, :].bitcast(I32))
+
+        def load_tab2():
+            for q in range(4):
+                nc.sync.dma_start(tab2_s[32 * q : 32 * q + 4, :].bitcast(I32), tab2_scales[0, 4 * q : 4 * q + 4, :].bitcast(I32))
+            load_words(tab2_w, tab2_words[0])
+
+        def load_slice(t):
+            for q in (0, 2, 1, 3):
+                nc.sync.dma_start(gain[t][32 * q : 32 * q + 32, :], wgs_rows[:, t, :])
+            nc.sync.dma_start(page[t][:], page_rows[:, t, :])
+
+        def load_avail():
+            with nc.allow_non_contiguous_dma(reason="one availability weight to a partition"):
+                nc.sync.dma_start(avail_sb[:], avail.rearrange("(n p) -> p n", p=P))
+
+        def load_w1():
+            nc.sync.dma_start(w1_raw[:].rearrange("p (a y) -> p a y", a=2), w1_words.rearrange("a p y -> p a y").bitcast(I32))
+
+        def load_w3():
+            nc.sync.dma_start(w3_raw[:].rearrange("p (a y) -> p a y", a=2), w3_words.rearrange("a p y i -> p a (y i)").bitcast(I32))
+
+        nc.sync.dma_start(list1[:], offs)
+        load_avail()
+        load_tab_scales()
+        load_words(tab_w[0], tab_words[0])
+        load_scales(w_s_rows, w1_scales, 0)
+        load_w2(0)
+        load_scales(w_s_rows, w3_scales, 4)
+        load_w2(1)
+        load_w1()
+        load_words(tab_w[1], tab_words[1])
+        load_w3()
+        nc.sync.dma_start(list3[:], offs3)
+        load_slice(0)
+        load_slice(1)
+        load_slice(2)
+        nc.sync.dma_start(list2[:], offs2)
+        nc.sync.dma_start(list4[:], offs4)
+        load_tab2()
+        load_slice(3)
+
+        root = held("root", [P, 4], F32)
+        inv_avail = held("inv_avail", [P, 4], F32)
+        nc.scalar.activation(root[:], avail_sb[:], ACT.Abs_reciprocal_sqrt)
+        nc.scalar.activation(inv_avail[:], root[:], ACT.Square)
+
+        v_s0 = held("v_s0", [P, S], U8)
+        nc.vector.tensor_copy(v_s0[:], tab_s[:].indirect(list1[:]))
+        nc.gpsimd.dma_start(v_s1[0:112, :].bitcast(I32), v_s0[4:116, :].bitcast(I32))
+        v_s = [v_s0[:], v_s0[4:]]
+        v_s_low = [v_s0[:], v_s1[:]]
+        v_w = [[held("v_w%d_%d" % (a, u), [P, N], I32) for u in range(2)] for a in range(2)]
+        for a in range(2):
+            for u in range(2):
+                nc.vector.tensor_copy(v_w[a][u][:].bitcast(U32), tab_w[a][:].bitcast(U32).indirect(list1[:, 32 * u : 32 * u + 32]))
+
+        w1_c = held("w1_c", [P, 2 * H // 2], I32)
+        nc.vector.tensor_copy(
+            w1_c[:].bitcast(U16).rearrange("p (a t m) -> p a m t", a=2, t=4),
+            w1_raw[:].bitcast(U16).rearrange("p (a m t) -> p a m t", a=2, t=4),
+        )
+        w3_c = held("w3_c", [P, 2 * H], I32)
+        nc.vector.tensor_copy(
+            w3_c[:].rearrange("p (a t m) -> p a m t", a=2, t=4),
+            w3_raw[:].rearrange("p (a m t) -> p a m t", a=2, t=4),
+        )
+        w_s = held("w_s", [P, 2 * H], U8)
+        nc.vector.tensor_copy(
+            w_s[:].rearrange("p (a t m) -> p a m t", a=2, t=4),
+            w_s_raw[:].rearrange("p (a m t) -> p a m t", a=2, t=4),
+        )
+        w2_g = [held("w2_g%d" % a, [P, 4 * H], BF16) for a in range(2)]
+        w2_c = [held("w2_c%d" % a, [P, H], I32) for a in range(2)]
+        w2_s = [held("w2_s%d" % a, [P, H], U8) for a in range(2)]
+        for a in range(2):
+            dst = w2_g[a][:].rearrange("p (t m j) -> p m j t", t=4, j=4)
+            src = w2_raw[a][:].rearrange("p j (m t) -> p m j t", t=4)
+            nc.scalar.copy(dst, src)
+            nc.vector.quantize_mx(w2_c[a][:].bitcast(FP8X4), w2_s[a][:], w2_g[a][:])
+
+        page_g = [held("page_g%d" % c, [P, N, 4], BF16) for c in range(4)]
+        w1_bytes = w1_c[:].bitcast(U8)
+        units = [(t, u) for t in range(4) for u in range(2)]
+        a_sb, acc_b, acc_c = {}, {}, {}
+
+        def product_a(t, u):
+            acc = bank("a")
+            for a in range(2):
+                c0 = H * a + P * t
+                nc.tensor.matmul_mx(
+                    acc[:], lhsT=w1_bytes[:, 2 * c0 : 2 * c0 + 2 * P].bitcast(FP4X4), lhsT_scale=w_s[:, c0 : c0 + P],
+                    rhs=v_w[a][u][:].bitcast(FP8X4), rhs_scale=v_s_low[a][:, N * u : N * (u + 1)], start=a == 0, stop=a == 1,
+                )
+            a_sb[t, u] = ring.tile([P, N], F32, name="a_sb", tag="ring_a")
+            nc.scalar.copy(a_sb[t, u][:], acc[:])
+
+        def products_bc(t, u):
+            acc_b[t, u] = bank("b")
+            for a in range(2):
+                nc.tensor.matmul_mx(
+                    acc_b[t, u][:], lhsT=w2_c[a][:, P * t : P * t + P].bitcast(FP8X4), lhsT_scale=w2_s[a][:, P * t : P * t + P],
+                    rhs=v_w[a][u][:].bitcast(FP8X4), rhs_scale=v_s[a][:, N * u : N * (u + 1)], start=a == 0, stop=a == 1,
+                )
+            acc_c[t, u] = bank("c")
+            for a in range(2):
+                c0 = H * a + P * t
+                nc.tensor.matmul_mx(
+                    acc_c[t, u][:], lhsT=w3_c[:, c0 : c0 + P].bitcast(FP8X4), lhsT_scale=w_s[4:, c0 : c0 + P],
+                    rhs=v_w[a][u][:].bitcast(FP8X4), rhs_scale=v_s[a][:, N * u : N * (u + 1)], start=a == 0, stop=a == 1,
+                )
+
+        def refill(t, u):
+            cols = slice(N * u, N * (u + 1))
+            least = ring.tile([P, N], F32, name="least", tag="least", bufs=2)
+            nc.vector.tensor_tensor(least[:], acc_b[t, u][:], a_sb[t, u][:], ALU.min)
+            h = ring.tile([P, N], F32, name="h", tag="h", bufs=2)
+            nc.vector.tensor_tensor(h[:], acc_c[t, u][:], least[:], ALU.mult)
+            nc.vector.tensor_tensor(page[t][:].indirect(list3[:, 32 * u : 32 * u + 32]), h[:], gain[t][:, cols], ALU.mult)
+
+        def round_slice(t):
+            for c in range(4):
+                src = page[t][:, N * c : N * (c + 1)]
+                if t == 2 and c < 2:
+                    nc.scalar.copy(page_g[c][:, :, 2:4], src.unsqueeze(2).to_broadcast([P, N, 2]))
+                elif t == 3 and c < 2:
+                    nc.vector.tensor_copy(page_g[c][:, :, t], src)
+                else:
+                    nc.scalar.copy(page_g[c][:, :, t], src)
+
+        v2_w = held("v2_w", [P, S2], I32)
+        v2_s = held("v2_s", [P, S2], U8)
+        for t, u in units:
+            product_a(t, u)
+            products_bc(t, u)
+            refill(t, u)
+            if t == 2 and u == 1:
+                nc.vector.tensor_copy(v2_w[:].bitcast(U32), tab2_w[:].bitcast(U32).indirect(list2[:]))
+                nc.vector.tensor_copy(v2_s[:], tab2_s[:].indirect(list2[:]))
+            if u == 1:
+                round_slice(t)
+
+        page_c = [held("page_c%d" % c, [P, N], I32) for c in range(4)]
+        page_s = [held("page_s%d" % c, [P, N], U8) for c in range(4)]
+        for c in range(4):
+            nc.vector.quantize_mx(page_c[c][:].bitcast(FP8X4), page_s[c][:], page_g[c][:].rearrange("p n t -> p (n t)"))
+
+        e = [held("e%d" % n, [P, T2], F32) for n in range(4)]
+        picked = {}
+        pieces = [[(0, 512), (512, 512)]] * 4
+
+        def product(n):
+            for c in range(4):
+                acc_e = bank("a")
+                nc.tensor.matmul_mx(
+                    acc_e[:], lhsT=v2_w[:, P * n : P * n + P].bitcast(FP8X4), lhsT_scale=v2_s[:, P * n : P * n + P],
+                    rhs=page_c[c][:].bitcast(FP8X4), rhs_scale=page_s[c][:], start=True, stop=True,
+                )
+                if (n == 0 and c >= 2) or (n >= 2 and c == 3):
+                    nc.vector.tensor_copy(e[n][:, N * c : N * (c + 1)], acc_e[:])
+                else:
+                    nc.scalar.copy(e[n][:, N * c : N * (c + 1)], acc_e[:])
+            for m0, width in pieces[n]:
+                x = ring.tile([P, width], F32, name="x", tag="ring_a")
+                nc.vector.tensor_copy(x[:], e[n][:].indirect(list4[:, m0 // 16 : (m0 + width) // 16]))
+                picked[n, m0] = x
+
+        def scores(n):
+            for m0, width in pieces[n]:
+                x2 = ring.tile([P, width], F32, name="x2", tag="least", bufs=2)
+                nc.scalar.activation(x2[:], picked[n, m0][:], ACT.Square)
+                r = ring.tile([P, width], F32, name="r", tag="ring_h")
+                nc.scalar.activation(r[:], x2[:], ACT.Abs_reciprocal_sqrt, bias=inv_avail[:, n : n + 1], scale=inv_avail[:, n : n + 1])
+                score = ring.tile([P, width], F32, name="score", tag="ring_h")
+                (nc.vector).tensor_tensor(score[:], r[:], r[:], ALU.mult)
+                nc.sync.dma_start(out[P * n : P * n + P, m0 : m0 + width], score[:])
+
+        product(0)
+        for n in range(4):
+            if n < 3:
+                product(n + 1)
+            scores(n)

@@ -80,10 +80,18 @@ def tile_list_tow_dispatch_scores_kernel(
                 nc.sync.dma_start(tab2_s[32 * q : 32 * q + 4, :].bitcast(I32), tab2_scales[0, 4 * q : 4 * q + 4, :].bitcast(I32))
             load_words(tab2_w, tab2_words[0])
 
-        def load_slice(t):
+        def load_gain(t, cols):
             for q in (0, 2, 1, 3):
-                nc.sync.dma_start(gain[t][32 * q : 32 * q + 32, :], wgs_rows[:, t, :])
-            nc.sync.dma_start(page[t][:], page_rows[:, t, :])
+                nc.sync.dma_start(gain[t][32 * q : 32 * q + 32, cols], wgs_rows[:, t, cols])
+
+        def load_slice(t):
+            if t == 0:
+                load_gain(t, slice(0, N))
+                nc.sync.dma_start(page[t][:], page_rows[:, t, :])
+                load_gain(t, slice(N, S))
+            else:
+                load_gain(t, slice(0, S))
+                nc.sync.dma_start(page[t][:], page_rows[:, t, :])
 
         def load_avail():
             with nc.allow_non_contiguous_dma(reason="one availability weight to a partition"):
@@ -157,7 +165,7 @@ def tile_list_tow_dispatch_scores_kernel(
         page_g = [held("page_g%d" % c, [P, N, 4], BF16) for c in range(4)]
         w1_bytes = w1_c[:].bitcast(U8)
         units = [(t, u) for t in range(4) for u in range(2)]
-        a_sb, acc_b, acc_c = {}, {}, {}
+        a_sb, acc_b, acc_c, c_sb = {}, {}, {}, {}
 
         def product_a(t, u):
             acc = bank("a")
@@ -185,13 +193,23 @@ def tile_list_tow_dispatch_scores_kernel(
                     rhs=v_w[a][u][:].bitcast(FP8X4), rhs_scale=v_s[a][:, N * u : N * (u + 1)], start=a == 0, stop=a == 1,
                 )
 
+            if (t, u) != units[0]:
+                c_sb[t, u] = ring.tile([P, N], F32, name="c_sb", tag="ring_h")
+                nc.scalar.copy(c_sb[t, u][:], acc_c[t, u][:])
+
         def refill(t, u):
             cols = slice(N * u, N * (u + 1))
-            least = ring.tile([P, N], F32, name="least", tag="least", bufs=2)
+            least = ring.tile([P, N], F32, name="least", tag="least", bufs=3)
             nc.vector.tensor_tensor(least[:], acc_b[t, u][:], a_sb[t, u][:], ALU.min)
-            h = ring.tile([P, N], F32, name="h", tag="h", bufs=2)
-            nc.vector.tensor_tensor(h[:], acc_c[t, u][:], least[:], ALU.mult)
-            nc.vector.tensor_tensor(page[t][:].indirect(list3[:, 32 * u : 32 * u + 32]), h[:], gain[t][:, cols], ALU.mult)
+            if (t, u) == units[0]:
+                h = ring.tile([P, N], F32, name="h", tag="ring_h")
+                nc.vector.tensor_tensor(h[:], acc_c[t, u][:], least[:], ALU.mult)
+                nc.vector.tensor_tensor(h[:], h[:], gain[t][:, cols], ALU.mult)
+            else:
+                h = c_sb[t, u]
+                nc.gpsimd.tensor_tensor(h[:], h[:], gain[t][:, cols], ALU.mult)
+                nc.gpsimd.tensor_tensor(h[:], h[:], least[:], ALU.mult)
+            nc.vector.tensor_copy(page[t][:].indirect(list3[:, 32 * u : 32 * u + 32]), h[:])
 
         def round_slice(t):
             for c in range(4):
@@ -231,7 +249,7 @@ def tile_list_tow_dispatch_scores_kernel(
                     acc_e[:], lhsT=v2_w[:, P * n : P * n + P].bitcast(FP8X4), lhsT_scale=v2_s[:, P * n : P * n + P],
                     rhs=page_c[c][:].bitcast(FP8X4), rhs_scale=page_s[c][:], start=True, stop=True,
                 )
-                if (n == 0 and c >= 2) or (n >= 2 and c == 3):
+                if c >= 2 and n != 1:
                     nc.vector.tensor_copy(e[n][:, N * c : N * (c + 1)], acc_e[:])
                 else:
                     nc.scalar.copy(e[n][:, N * c : N * (c + 1)], acc_e[:])
@@ -242,12 +260,12 @@ def tile_list_tow_dispatch_scores_kernel(
 
         def scores(n):
             for m0, width in pieces[n]:
-                x2 = ring.tile([P, width], F32, name="x2", tag="least", bufs=2)
+                x2 = ring.tile([P, width], F32, name="x2", tag="least", bufs=3)
                 nc.scalar.activation(x2[:], picked[n, m0][:], ACT.Square)
                 r = ring.tile([P, width], F32, name="r", tag="ring_h")
                 nc.scalar.activation(r[:], x2[:], ACT.Abs_reciprocal_sqrt, bias=inv_avail[:, n : n + 1], scale=inv_avail[:, n : n + 1])
                 score = ring.tile([P, width], F32, name="score", tag="ring_h")
-                (nc.vector).tensor_tensor(score[:], r[:], r[:], ALU.mult)
+                (nc.gpsimd if n < 3 else nc.vector).tensor_tensor(score[:], r[:], r[:], ALU.mult)
                 nc.sync.dma_start(out[P * n : P * n + P, m0 : m0 + width], score[:])
 
         product(0)

@@ -2,7 +2,7 @@ from contextlib import ExitStack
 
 import concourse.mybir as mybir
 
-K, T, S, H, T2, T3, S2, PK = 1024, 2048, 1024, 512, 2048, 2048, 512, 1024
+K, T, S, H, T2, T3, S2, PICKED = 1024, 2048, 1024, 512, 2048, 2048, 512, 1024
 FLOPS = 2 * (3 * K * H * S + H * S2 * T2)
 
 F32 = mybir.dt.float32
@@ -18,6 +18,20 @@ ACT = mybir.ActivationFunctionType
 
 P = 128
 N = 512
+PACK = 4
+PASSES = K // (P * PACK)
+HALVES = S // N
+CHUNKS = T2 // N
+GROUPS = S2 // P
+QUADRANTS = 4
+LIST_COLS = N // 16
+
+PIECES = PACK * HALVES
+FILL_BUFS = 3
+BANKS = {"a": 4, "b": 2, "c": 2}
+VECTOR_CHUNKS = 2
+FIRST_SQUARES = {"gpsimd": 3, "scalar": 3}
+SECOND_SQUARES = {"gpsimd": 2, "scalar": 1}
 
 
 def tile_list_tow_dispatch_scores_kernel(
@@ -27,104 +41,91 @@ def tile_list_tow_dispatch_scores_kernel(
     nc = tc.nc
     with ExitStack() as ctx:
         keep = ctx.enter_context(tc.tile_pool(name="keep", bufs=1))
-        ring = ctx.enter_context(tc.tile_pool(name="ring", bufs=8))
+        ring = ctx.enter_context(tc.tile_pool(name="ring", bufs=PIECES))
         psum = ctx.enter_context(tc.psum_pool(name="psum", bufs=1))
-        banks = {"a": 4, "b": 2, "c": 2}
 
         def bank(tag):
-            return psum.tile([P, N], F32, name="acc_" + tag, tag=tag, bufs=banks[tag])
+            return psum.tile([P, N], F32, name="acc_" + tag, tag=tag, bufs=BANKS[tag])
 
         def held(name, shape, dtype):
             return keep.tile(shape, dtype, name=name, align_bytes=64)
 
+        def span(i, width):
+            return slice(width * i, width * (i + 1))
+
         list1 = held("list1", [P, S // 16], U16)
         list2 = held("list2", [P, S2 // 16], U16)
         list3 = held("list3", [P, S // 16], U16)
-        list4 = held("list4", [P, PK // 16], U16)
+        list4 = held("list4", [P, PICKED // 16], U16)
 
         tab_s = held("tab_s", [P, T], U8)
         v_s1 = held("v_s1", [P, S], U8)
-        w_s_raw = held("w_s_raw", [P, 2 * H], U8)
+        w_s_raw = held("w_s_raw", [P, PASSES * H], U8)
         tab2_s = held("tab2_s", [P, T3], U8)
-        for plane in (tab_s, w_s_raw, v_s1, tab2_s):
-            nc.vector.memset(plane[:].bitcast(I32), 0)
+        nc.vector.memset(tab_s[:, span(0, T // 2)].bitcast(I32), 0)
+        nc.gpsimd.memset(tab_s[:, span(1, T // 2)].bitcast(I32), 0)
+        nc.gpsimd.memset(tab2_s[:].bitcast(I32), 0)
+        for scales in (w_s_raw, v_s1):
+            nc.vector.memset(scales[:].bitcast(I32), 0)
 
-        tab_w = [held("tab_w%d" % a, [P, T], I32) for a in range(2)]
-        w1_raw = held("w1_raw", [P, 2 * H // 2], I32)
-        avail_sb = held("avail_sb", [P, 4], F32)
-        w_s_rows = w_s_raw[:].bitcast(I32).rearrange("p (a y) -> p a y", a=2)
-        w2_raw = [held("w2_raw%d" % a, [P, 4, H], F32) for a in range(2)]
-        w3_raw = held("w3_raw", [P, 2 * H], I32)
-        wgs_rows = wgs.rearrange("(m t) j -> m t j", t=4)
-        page_rows = page0.rearrange("(p t) c -> p t c", t=4)
-        gain = [held("gain%d" % t, [P, S], F32) for t in range(4)]
-        page = [held("page%d" % t, [P, T2], F32) for t in range(4)]
+        tab_w = [held("tab_w%d" % g, [P, T], I32) for g in range(PASSES)]
+        w1_raw = held("w1_raw", [P, PASSES * H // 2], I32)
+        avail_sb = held("avail_sb", [P, GROUPS], F32)
+        w2_raw = [held("w2_raw%d" % g, [P, PACK, H], F32) for g in range(PASSES)]
+        w3_raw = held("w3_raw", [P, PASSES * H], I32)
+        gain = [held("gain%d" % t, [P, S], F32) for t in range(PACK)]
+        page = [held("page%d" % t, [P, T2], F32) for t in range(PACK)]
         tab2_w = held("tab2_w", [P, T3], I32)
 
         def load_words(tile, words):
             nc.sync.dma_start(tile[:], words.rearrange("p t i -> p (t i)").bitcast(I32))
 
-        def load_w2(a):
-            nc.sync.dma_start(w2_raw[a][:], w2[512 * a : 512 * (a + 1), :].rearrange("(p j) y -> p j y", j=4))
+        def load_w2(g):
+            nc.sync.dma_start(w2_raw[g][:], w2[span(g, P * PACK), :].rearrange("(p i) r -> p i r", i=PACK))
 
-        def load_scales(rows, scales, first):
-            for q in range(4):
-                nc.sync.dma_start(rows[32 * q + first : 32 * q + first + 4], scales[:, 4 * q : 4 * q + 4, :].rearrange("a q y -> q a y").bitcast(I32))
+        def load_weight_scales(scales, first):
+            rows = w_s_raw[:].bitcast(I32).rearrange("p (g r) -> p g r", g=PASSES)
+            for q in range(QUADRANTS):
+                source = scales[:, span(q, 4), :].rearrange("g b r -> b g r")
+                nc.sync.dma_start(rows[32 * q + first : 32 * q + first + 4], source.bitcast(I32))
 
-        def load_tab_scales():
-            for q in range(4):
-                nc.sync.dma_start(tab_s[32 * q : 32 * q + 8, :].bitcast(I32), tab_scales[:, 4 * q : 4 * q + 4, :].bitcast(I32))
-
-        def load_tab2():
-            for q in range(4):
-                nc.sync.dma_start(tab2_s[32 * q : 32 * q + 4, :].bitcast(I32), tab2_scales[0, 4 * q : 4 * q + 4, :].bitcast(I32))
-            load_words(tab2_w, tab2_words[0])
-
-        def load_gain(t, cols):
+        def load_gain(t, half):
+            rows = wgs.rearrange("(m t) j -> m t j", t=PACK)
             for q in (0, 2, 1, 3):
-                nc.sync.dma_start(gain[t][32 * q : 32 * q + 32, cols], wgs_rows[:, t, cols])
-
-        def load_slice(t):
-            if t == 0:
-                load_gain(t, slice(0, N))
-                nc.sync.dma_start(page[t][:], page_rows[:, t, :])
-                load_gain(t, slice(N, S))
-            else:
-                load_gain(t, slice(0, S))
-                nc.sync.dma_start(page[t][:], page_rows[:, t, :])
-
-        def load_avail():
-            with nc.allow_non_contiguous_dma(reason="one availability weight to a partition"):
-                nc.sync.dma_start(avail_sb[:], avail.rearrange("(n p) -> p n", p=P))
-
-        def load_w1():
-            nc.sync.dma_start(w1_raw[:].rearrange("p (a y) -> p a y", a=2), w1_words.rearrange("a p y -> p a y").bitcast(I32))
-
-        def load_w3():
-            nc.sync.dma_start(w3_raw[:].rearrange("p (a y) -> p a y", a=2), w3_words.rearrange("a p y i -> p a (y i)").bitcast(I32))
+                nc.sync.dma_start(gain[t][span(q, 32), span(half, N)], rows[:, t, span(half, N)])
 
         nc.sync.dma_start(list1[:], offs)
-        load_avail()
-        load_tab_scales()
+        with nc.allow_non_contiguous_dma(reason="one availability weight to a partition and group"):
+            nc.scalar.dma_start(avail_sb[:], avail.rearrange("(n p) -> p n", p=P))
+        for q in range(QUADRANTS):
+            nc.sync.dma_start(tab_s[32 * q : 32 * q + 8, :].bitcast(I32), tab_scales[:, span(q, 4), :].bitcast(I32))
+        for q in range(QUADRANTS):
+            nc.gpsimd.dma_start(tab2_s[32 * q : 32 * q + 4, :].bitcast(I32), tab2_scales[0, span(q, 4), :].bitcast(I32))
         load_words(tab_w[0], tab_words[0])
-        load_scales(w_s_rows, w1_scales, 0)
+        load_weight_scales(w1_scales, 0)
         load_w2(0)
-        load_scales(w_s_rows, w3_scales, 4)
-        load_w2(1)
-        load_w1()
-        load_words(tab_w[1], tab_words[1])
-        load_w3()
-        nc.sync.dma_start(list3[:], offs3)
-        load_slice(0)
-        load_slice(1)
-        load_slice(2)
         nc.sync.dma_start(list2[:], offs2)
+        load_weight_scales(w3_scales, 4)
+        load_w2(1)
+        nc.sync.dma_start(list3[:], offs3)
+        nc.sync.dma_start(
+            w1_raw[:].rearrange("p (g r) -> p g r", g=PASSES), w1_words.rearrange("g p r -> p g r").bitcast(I32)
+        )
+        load_words(tab_w[1], tab_words[1])
+        nc.sync.dma_start(
+            w3_raw[:].rearrange("p (g r) -> p g r", g=PASSES), w3_words.rearrange("g p r i -> p g (r i)").bitcast(I32)
+        )
+        page_rows = page0.rearrange("(p t) c -> p t c", t=PACK)
+        for t in range(PACK):
+            load_gain(t, 0)
+            nc.sync.dma_start(page[t][:], page_rows[:, t, :])
+            if t == PACK - 1:
+                load_words(tab2_w, tab2_words[0])
+            load_gain(t, 1)
         nc.sync.dma_start(list4[:], offs4)
-        load_tab2()
-        load_slice(3)
 
-        root = held("root", [P, 4], F32)
-        inv_avail = held("inv_avail", [P, 4], F32)
+        root = held("root", [P, GROUPS], F32)
+        inv_avail = held("inv_avail", [P, GROUPS], F32)
         nc.scalar.activation(root[:], avail_sb[:], ACT.Abs_reciprocal_sqrt)
         nc.scalar.activation(inv_avail[:], root[:], ACT.Square)
 
@@ -132,144 +133,137 @@ def tile_list_tow_dispatch_scores_kernel(
         nc.vector.tensor_copy(v_s0[:], tab_s[:].indirect(list1[:]))
         nc.gpsimd.dma_start(v_s1[0:112, :].bitcast(I32), v_s0[4:116, :].bitcast(I32))
         v_s = [v_s0[:], v_s0[4:]]
-        v_s_low = [v_s0[:], v_s1[:]]
-        v_w = [[held("v_w%d_%d" % (a, u), [P, N], I32) for u in range(2)] for a in range(2)]
-        for a in range(2):
-            for u in range(2):
-                nc.vector.tensor_copy(v_w[a][u][:].bitcast(U32), tab_w[a][:].bitcast(U32).indirect(list1[:, 32 * u : 32 * u + 32]))
+        v_s_from_row0 = [v_s0[:], v_s1[:]]
+        v_w = [[held("v_w%d_%d" % (g, half), [P, N], I32) for half in range(HALVES)] for g in range(PASSES)]
+        for g in range(PASSES):
+            for half in range(HALVES):
+                window = tab_w[g][:].bitcast(U32)
+                nc.vector.tensor_copy(v_w[g][half][:].bitcast(U32), window.indirect(list1[:, span(half, LIST_COLS)]))
 
-        w1_c = held("w1_c", [P, 2 * H // 2], I32)
-        nc.vector.tensor_copy(
-            w1_c[:].bitcast(U16).rearrange("p (a t m) -> p a m t", a=2, t=4),
-            w1_raw[:].bitcast(U16).rearrange("p (a m t) -> p a m t", a=2, t=4),
-        )
-        w3_c = held("w3_c", [P, 2 * H], I32)
-        nc.vector.tensor_copy(
-            w3_c[:].rearrange("p (a t m) -> p a m t", a=2, t=4),
-            w3_raw[:].rearrange("p (a m t) -> p a m t", a=2, t=4),
-        )
-        w_s = held("w_s", [P, 2 * H], U8)
-        nc.vector.tensor_copy(
-            w_s[:].rearrange("p (a t m) -> p a m t", a=2, t=4),
-            w_s_raw[:].rearrange("p (a m t) -> p a m t", a=2, t=4),
-        )
-        w2_g = [held("w2_g%d" % a, [P, 4 * H], BF16) for a in range(2)]
-        w2_c = [held("w2_c%d" % a, [P, H], I32) for a in range(2)]
-        w2_s = [held("w2_s%d" % a, [P, H], U8) for a in range(2)]
-        for a in range(2):
-            dst = w2_g[a][:].rearrange("p (t m j) -> p m j t", t=4, j=4)
-            src = w2_raw[a][:].rearrange("p j (m t) -> p m j t", t=4)
-            nc.scalar.copy(dst, src)
-            nc.vector.quantize_mx(w2_c[a][:].bitcast(FP8X4), w2_s[a][:], w2_g[a][:])
+        def reorder_columns(ordered, raw):
+            nc.vector.tensor_copy(
+                ordered.rearrange("p (g t m) -> p g m t", g=PASSES, t=PACK),
+                raw.rearrange("p (g m t) -> p g m t", g=PASSES, t=PACK),
+            )
 
-        page_g = [held("page_g%d" % c, [P, N, 4], BF16) for c in range(4)]
+        w1_c = held("w1_c", [P, PASSES * H // 2], I32)
+        reorder_columns(w1_c[:].bitcast(U16), w1_raw[:].bitcast(U16))
+        w3_c = held("w3_c", [P, PASSES * H], I32)
+        reorder_columns(w3_c[:], w3_raw[:])
+        w_s = held("w_s", [P, PASSES * H], U8)
+        reorder_columns(w_s[:], w_s_raw[:])
+
+        w2_rounded = [held("w2_rounded%d" % g, [P, PACK * H], BF16) for g in range(PASSES)]
+        w2_c = [held("w2_c%d" % g, [P, H], I32) for g in range(PASSES)]
+        w2_s = [held("w2_s%d" % g, [P, H], U8) for g in range(PASSES)]
+        for g in range(PASSES):
+            nc.scalar.copy(
+                w2_rounded[g][:].rearrange("p (t m i) -> p m i t", t=PACK, i=PACK),
+                w2_raw[g][:].rearrange("p i (m t) -> p m i t", t=PACK),
+            )
+            nc.vector.quantize_mx(w2_c[g][:].bitcast(FP8X4), w2_s[g][:], w2_rounded[g][:])
+
+        page_rounded = [held("page_rounded%d" % c, [P, N, PACK], BF16) for c in range(CHUNKS)]
         w1_bytes = w1_c[:].bitcast(U8)
-        units = [(t, u) for t in range(4) for u in range(2)]
-        a_sb, acc_b, acc_c, c_sb = {}, {}, {}, {}
 
-        def product_a(t, u):
-            acc = bank("a")
-            for a in range(2):
-                c0 = H * a + P * t
+        def product(tag, half, codes, scales, v_scales):
+            acc = bank(tag)
+            for g in range(PASSES):
                 nc.tensor.matmul_mx(
-                    acc[:], lhsT=w1_bytes[:, 2 * c0 : 2 * c0 + 2 * P].bitcast(FP4X4), lhsT_scale=w_s[:, c0 : c0 + P],
-                    rhs=v_w[a][u][:].bitcast(FP8X4), rhs_scale=v_s_low[a][:, N * u : N * (u + 1)], start=a == 0, stop=a == 1,
+                    acc[:], lhsT=codes[g], lhsT_scale=scales[g], rhs=v_w[g][half][:].bitcast(FP8X4),
+                    rhs_scale=v_scales[g][:, span(half, N)], start=g == 0, stop=g == PASSES - 1,
                 )
-            a_sb[t, u] = ring.tile([P, N], F32, name="a_sb", tag="ring_a")
-            nc.scalar.copy(a_sb[t, u][:], acc[:])
+            return acc
 
-        def products_bc(t, u):
-            acc_b[t, u] = bank("b")
-            for a in range(2):
-                nc.tensor.matmul_mx(
-                    acc_b[t, u][:], lhsT=w2_c[a][:, P * t : P * t + P].bitcast(FP8X4), lhsT_scale=w2_s[a][:, P * t : P * t + P],
-                    rhs=v_w[a][u][:].bitcast(FP8X4), rhs_scale=v_s[a][:, N * u : N * (u + 1)], start=a == 0, stop=a == 1,
-                )
-            acc_c[t, u] = bank("c")
-            for a in range(2):
-                c0 = H * a + P * t
-                nc.tensor.matmul_mx(
-                    acc_c[t, u][:], lhsT=w3_c[:, c0 : c0 + P].bitcast(FP8X4), lhsT_scale=w_s[4:, c0 : c0 + P],
-                    rhs=v_w[a][u][:].bitcast(FP8X4), rhs_scale=v_s[a][:, N * u : N * (u + 1)], start=a == 0, stop=a == 1,
-                )
-
-            if (t, u) != units[0]:
-                c_sb[t, u] = ring.tile([P, N], F32, name="c_sb", tag="ring_h")
-                nc.scalar.copy(c_sb[t, u][:], acc_c[t, u][:])
-
-        def refill(t, u):
-            cols = slice(N * u, N * (u + 1))
-            least = ring.tile([P, N], F32, name="least", tag="least", bufs=3)
-            nc.vector.tensor_tensor(least[:], acc_b[t, u][:], a_sb[t, u][:], ALU.min)
-            if (t, u) == units[0]:
-                h = ring.tile([P, N], F32, name="h", tag="ring_h")
-                nc.vector.tensor_tensor(h[:], acc_c[t, u][:], least[:], ALU.mult)
-                nc.vector.tensor_tensor(h[:], h[:], gain[t][:, cols], ALU.mult)
+        def refill(t, half):
+            blocks = [PACK * g + t for g in range(PASSES)]
+            acc_a = product(
+                "a", half, [w1_bytes[:, span(b, 2 * P)].bitcast(FP4X4) for b in blocks],
+                [w_s[:, span(b, P)] for b in blocks], v_s_from_row0,
+            )
+            a_sb = ring.tile([P, N], F32, name="a_sb", tag="a_then_x")
+            nc.scalar.copy(a_sb[:], acc_a[:])
+            acc_b = product(
+                "b", half, [w2_c[g][:, span(t, P)].bitcast(FP8X4) for g in range(PASSES)],
+                [w2_s[g][:, span(t, P)] for g in range(PASSES)], v_s,
+            )
+            acc_c = product(
+                "c", half, [w3_c[:, span(b, P)].bitcast(FP8X4) for b in blocks],
+                [w_s[4:, span(b, P)] for b in blocks], v_s,
+            )
+            first_piece = t == 0 and half == 0
+            if not first_piece:
+                c_sb = ring.tile([P, N], F32, name="c_sb")
+                nc.scalar.copy(c_sb[:], acc_c[:])
+            weights = gain[t][:, span(half, N)]
+            fill = ring.tile([P, N], F32, name="fill", bufs=FILL_BUFS)
+            nc.vector.tensor_tensor(fill[:], acc_b[:], a_sb[:], ALU.min)
+            if first_piece:
+                nc.vector.tensor_tensor(fill[:], acc_c[:], fill[:], ALU.mult)
+                nc.vector.tensor_tensor(fill[:], fill[:], weights, ALU.mult)
             else:
-                h = c_sb[t, u]
-                nc.gpsimd.tensor_tensor(h[:], h[:], gain[t][:, cols], ALU.mult)
-                nc.gpsimd.tensor_tensor(h[:], h[:], least[:], ALU.mult)
-            nc.vector.tensor_copy(page[t][:].indirect(list3[:, 32 * u : 32 * u + 32]), h[:])
+                nc.gpsimd.tensor_tensor(c_sb[:], c_sb[:], weights, ALU.mult)
+                nc.gpsimd.tensor_tensor(fill[:], fill[:], c_sb[:], ALU.mult)
+            nc.vector.tensor_copy(page[t][:].indirect(list3[:, span(half, LIST_COLS)]), fill[:])
 
         def round_slice(t):
-            for c in range(4):
-                src = page[t][:, N * c : N * (c + 1)]
-                if t == 2 and c < 2:
-                    nc.scalar.copy(page_g[c][:, :, 2:4], src.unsqueeze(2).to_broadcast([P, N, 2]))
-                elif t == 3 and c < 2:
-                    nc.vector.tensor_copy(page_g[c][:, :, t], src)
+            for c in range(CHUNKS):
+                source = page[t][:, span(c, N)]
+                if t == PACK - 2 and c < VECTOR_CHUNKS:
+                    nc.scalar.copy(page_rounded[c][:, :, t : t + 2], source.unsqueeze(2).to_broadcast([P, N, 2]))
+                elif t == PACK - 1 and c < VECTOR_CHUNKS:
+                    nc.vector.tensor_copy(page_rounded[c][:, :, t], source)
                 else:
-                    nc.scalar.copy(page_g[c][:, :, t], src)
+                    nc.scalar.copy(page_rounded[c][:, :, t], source)
 
         v2_w = held("v2_w", [P, S2], I32)
         v2_s = held("v2_s", [P, S2], U8)
-        for t, u in units:
-            product_a(t, u)
-            products_bc(t, u)
-            refill(t, u)
-            if t == 2 and u == 1:
+        for t in range(PACK):
+            for half in range(HALVES):
+                refill(t, half)
+            if t == PACK - 2:
                 nc.vector.tensor_copy(v2_w[:].bitcast(U32), tab2_w[:].bitcast(U32).indirect(list2[:]))
                 nc.vector.tensor_copy(v2_s[:], tab2_s[:].indirect(list2[:]))
-            if u == 1:
-                round_slice(t)
+            round_slice(t)
 
-        page_c = [held("page_c%d" % c, [P, N], I32) for c in range(4)]
-        page_s = [held("page_s%d" % c, [P, N], U8) for c in range(4)]
-        for c in range(4):
-            nc.vector.quantize_mx(page_c[c][:].bitcast(FP8X4), page_s[c][:], page_g[c][:].rearrange("p n t -> p (n t)"))
+        page_c = [held("page_c%d" % c, [P, N], I32) for c in range(CHUNKS)]
+        page_s = [held("page_s%d" % c, [P, N], U8) for c in range(CHUNKS)]
+        for c in range(CHUNKS):
+            words = page_rounded[c][:].rearrange("p n t -> p (n t)")
+            nc.vector.quantize_mx(page_c[c][:].bitcast(FP8X4), page_s[c][:], words)
 
-        e = [held("e%d" % n, [P, T2], F32) for n in range(4)]
-        picked = {}
-        pieces = [[(0, 512), (512, 512)]] * 4
-
-        def product(n):
-            for c in range(4):
+        e = [held("e%d" % n, [P, T2], F32) for n in range(GROUPS)]
+        picked = []
+        for n in range(GROUPS):
+            for c in range(CHUNKS):
                 acc_e = bank("a")
                 nc.tensor.matmul_mx(
-                    acc_e[:], lhsT=v2_w[:, P * n : P * n + P].bitcast(FP8X4), lhsT_scale=v2_s[:, P * n : P * n + P],
+                    acc_e[:], lhsT=v2_w[:, span(n, P)].bitcast(FP8X4), lhsT_scale=v2_s[:, span(n, P)],
                     rhs=page_c[c][:].bitcast(FP8X4), rhs_scale=page_s[c][:], start=True, stop=True,
                 )
-                if c >= 2 and n != 1:
-                    nc.vector.tensor_copy(e[n][:, N * c : N * (c + 1)], acc_e[:])
+                if n == 0 and c >= CHUNKS - VECTOR_CHUNKS:
+                    nc.vector.tensor_copy(e[n][:, span(c, N)], acc_e[:])
                 else:
-                    nc.scalar.copy(e[n][:, N * c : N * (c + 1)], acc_e[:])
-            for m0, width in pieces[n]:
-                x = ring.tile([P, width], F32, name="x", tag="ring_a")
-                nc.vector.tensor_copy(x[:], e[n][:].indirect(list4[:, m0 // 16 : (m0 + width) // 16]))
-                picked[n, m0] = x
+                    nc.scalar.copy(e[n][:, span(c, N)], acc_e[:])
+            for half in range(HALVES):
+                x = ring.tile([P, N], F32, name="x", tag="a_then_x")
+                nc.vector.tensor_copy(x[:], e[n][:].indirect(list4[:, span(half, LIST_COLS)]))
+                picked.append((n, half, x))
 
-        def scores(n):
-            for m0, width in pieces[n]:
-                x2 = ring.tile([P, width], F32, name="x2", tag="least", bufs=3)
-                nc.scalar.activation(x2[:], picked[n, m0][:], ACT.Square)
-                r = ring.tile([P, width], F32, name="r", tag="ring_h")
-                nc.scalar.activation(r[:], x2[:], ACT.Abs_reciprocal_sqrt, bias=inv_avail[:, n : n + 1], scale=inv_avail[:, n : n + 1])
-                score = ring.tile([P, width], F32, name="score", tag="ring_h")
-                (nc.gpsimd if n < 3 else nc.vector).tensor_tensor(score[:], r[:], r[:], ALU.mult)
-                nc.sync.dma_start(out[P * n : P * n + P, m0 : m0 + width], score[:])
+        def square(x, piece, shares):
+            if piece < shares["gpsimd"]:
+                nc.gpsimd.tensor_tensor(x[:], x[:], x[:], ALU.mult)
+            elif piece < shares["gpsimd"] + shares["scalar"]:
+                nc.scalar.activation(x[:], x[:], ACT.Square)
+            else:
+                nc.vector.tensor_tensor(x[:], x[:], x[:], ALU.mult)
 
-        product(0)
-        for n in range(4):
-            if n < 3:
-                product(n + 1)
-            scores(n)
+        for piece in range(FIRST_SQUARES["gpsimd"]):
+            square(picked[piece][2], piece, FIRST_SQUARES)
+        for piece, (n, half, x) in enumerate(picked):
+            if piece >= FIRST_SQUARES["gpsimd"]:
+                square(x, piece, FIRST_SQUARES)
+            factor = inv_avail[:, n : n + 1]
+            nc.scalar.activation(x[:], x[:], ACT.Abs_reciprocal_sqrt, bias=factor, scale=factor)
+            square(x, piece, SECOND_SQUARES)
+            nc.sync.dma_start(out[span(n, P), span(half, N)], x[:])

@@ -27,11 +27,10 @@ QUADRANTS = 4
 LIST_COLS = N // 16
 
 PIECES = PACK * HALVES
-FILL_BUFS = 3
-BANKS = {"a": 4, "b": 2, "c": 2}
+BANKS = {"a": (0, 1), "b": (2, 3, 4), "c": (5, 6, 7)}
 VECTOR_CHUNKS = 2
-FIRST_SQUARES = {"gpsimd": 3, "scalar": 3}
-SECOND_SQUARES = {"gpsimd": 2, "scalar": 1}
+FIRST_SQUARES = {"gpsimd": 6, "scalar": 0}
+SECOND_SQUARES = {"gpsimd": 0, "scalar": 4}
 
 
 def tile_list_tow_dispatch_scores_kernel(
@@ -44,11 +43,11 @@ def tile_list_tow_dispatch_scores_kernel(
         ring = ctx.enter_context(tc.tile_pool(name="ring", bufs=PIECES))
         psum = ctx.enter_context(tc.psum_pool(name="psum", bufs=1))
 
-        def bank(tag):
-            return psum.tile([P, N], F32, name="acc_" + tag, tag=tag, bufs=BANKS[tag])
+        def bank(number):
+            return psum.tile([P, N], F32, name="acc", tag="bank%d" % number)
 
-        def held(name, shape, dtype):
-            return keep.tile(shape, dtype, name=name, align_bytes=64)
+        def held(name, shape, dtype, tag=None):
+            return keep.tile(shape, dtype, name=name, tag=tag or name, align_bytes=64)
 
         def span(i, width):
             return slice(width * i, width * (i + 1))
@@ -60,12 +59,13 @@ def tile_list_tow_dispatch_scores_kernel(
 
         tab_s = held("tab_s", [P, T], U8)
         v_s1 = held("v_s1", [P, S], U8)
-        w_s_raw = held("w_s_raw", [P, PASSES * H], U8)
+        w1_s_raw = held("w1_s_raw", [P, PASSES * H], U8)
+        w3_s_raw = held("w3_s_raw", [P, PASSES * H], U8)
         tab2_s = held("tab2_s", [P, T3], U8)
         nc.vector.memset(tab_s[:, span(0, T // 2)].bitcast(I32), 0)
         nc.gpsimd.memset(tab_s[:, span(1, T // 2)].bitcast(I32), 0)
         nc.gpsimd.memset(tab2_s[:].bitcast(I32), 0)
-        for scales in (w_s_raw, v_s1):
+        for scales in (w1_s_raw, w3_s_raw, v_s1):
             nc.vector.memset(scales[:].bitcast(I32), 0)
 
         tab_w = [held("tab_w%d" % g, [P, T], I32) for g in range(PASSES)]
@@ -83,11 +83,11 @@ def tile_list_tow_dispatch_scores_kernel(
         def load_w2(g):
             nc.sync.dma_start(w2_raw[g][:], w2[span(g, P * PACK), :].rearrange("(p i) r -> p i r", i=PACK))
 
-        def load_weight_scales(scales, first):
-            rows = w_s_raw[:].bitcast(I32).rearrange("p (g r) -> p g r", g=PASSES)
+        def load_weight_scales(tile, scales):
+            rows = tile[:].bitcast(I32).rearrange("p (g r) -> p g r", g=PASSES)
             for q in range(QUADRANTS):
                 source = scales[:, span(q, 4), :].rearrange("g b r -> b g r")
-                nc.sync.dma_start(rows[32 * q + first : 32 * q + first + 4], source.bitcast(I32))
+                nc.sync.dma_start(rows[32 * q : 32 * q + 4], source.bitcast(I32))
 
         def load_gain(t, half):
             rows = wgs.rearrange("(m t) j -> m t j", t=PACK)
@@ -99,27 +99,31 @@ def tile_list_tow_dispatch_scores_kernel(
             nc.scalar.dma_start(avail_sb[:], avail.rearrange("(n p) -> p n", p=P))
         for q in range(QUADRANTS):
             nc.sync.dma_start(tab_s[32 * q : 32 * q + 8, :].bitcast(I32), tab_scales[:, span(q, 4), :].bitcast(I32))
-        for q in range(QUADRANTS):
-            nc.gpsimd.dma_start(tab2_s[32 * q : 32 * q + 4, :].bitcast(I32), tab2_scales[0, span(q, 4), :].bitcast(I32))
         load_words(tab_w[0], tab_words[0])
-        load_weight_scales(w1_scales, 0)
+        load_words(tab_w[1], tab_words[1])
+        load_weight_scales(w1_s_raw, w1_scales)
         load_w2(0)
-        nc.sync.dma_start(list2[:], offs2)
-        load_weight_scales(w3_scales, 4)
-        load_w2(1)
-        nc.sync.dma_start(list3[:], offs3)
         nc.sync.dma_start(
             w1_raw[:].rearrange("p (g r) -> p g r", g=PASSES), w1_words.rearrange("g p r -> p g r").bitcast(I32)
         )
-        load_words(tab_w[1], tab_words[1])
+        v_s0 = held("v_s0", [P, S], U8)
+        nc.vector.tensor_copy(v_s0[:], tab_s[:].indirect(list1[:]))
+        nc.sync.dma_start(v_s1[0:112, :].bitcast(I32), v_s0[4:116, :].bitcast(I32))
+        load_weight_scales(w3_s_raw, w3_scales)
+        load_w2(1)
         nc.sync.dma_start(
             w3_raw[:].rearrange("p (g r) -> p g r", g=PASSES), w3_words.rearrange("g p r i -> p g (r i)").bitcast(I32)
         )
+        nc.sync.dma_start(list3[:], offs3)
         page_rows = page0.rearrange("(p t) c -> p t c", t=PACK)
         for t in range(PACK):
             load_gain(t, 0)
             nc.sync.dma_start(page[t][:], page_rows[:, t, :])
             if t == PACK - 1:
+                nc.sync.dma_start(list2[:], offs2)
+                for q in range(QUADRANTS):
+                    rows = tab2_scales[0, span(q, 4), :]
+                    nc.sync.dma_start(tab2_s[32 * q : 32 * q + 4, :].bitcast(I32), rows.bitcast(I32))
                 load_words(tab2_w, tab2_words[0])
             load_gain(t, 1)
         nc.sync.dma_start(list4[:], offs4)
@@ -129,9 +133,6 @@ def tile_list_tow_dispatch_scores_kernel(
         nc.scalar.activation(root[:], avail_sb[:], ACT.Abs_reciprocal_sqrt)
         nc.scalar.activation(inv_avail[:], root[:], ACT.Square)
 
-        v_s0 = held("v_s0", [P, S], U8)
-        nc.vector.tensor_copy(v_s0[:], tab_s[:].indirect(list1[:]))
-        nc.gpsimd.dma_start(v_s1[0:112, :].bitcast(I32), v_s0[4:116, :].bitcast(I32))
         v_s = [v_s0[:], v_s0[4:]]
         v_s_from_row0 = [v_s0[:], v_s1[:]]
         v_w = [[held("v_w%d_%d" % (g, half), [P, N], I32) for half in range(HALVES)] for g in range(PASSES)]
@@ -146,28 +147,54 @@ def tile_list_tow_dispatch_scores_kernel(
                 raw.rearrange("p (g m t) -> p g m t", g=PASSES, t=PACK),
             )
 
-        w1_c = held("w1_c", [P, PASSES * H // 2], I32)
-        reorder_columns(w1_c[:].bitcast(U16), w1_raw[:].bitcast(U16))
+        w1_cols = w1_raw[:].bitcast(U16).rearrange("p (g m t) -> p g m t", g=PASSES, t=PACK)
+        w1_c = {}
+
+        def order_w1(first, count, tag):
+            tile = held("w1_c", [P, count * PASSES * P // 2], I32, tag)
+            ordered = tile[:].bitcast(U16).rearrange("p (t g m) -> p g m t", g=PASSES, t=count)
+            nc.vector.tensor_copy(ordered, w1_cols[:, :, :, first : first + count])
+            for t in range(count):
+                w1_c[first + t] = tile[:].bitcast(U8)[:, span(t, PASSES * 2 * P)]
+
+        def w1_slice(t, g):
+            return w1_c[t][:, span(g, 2 * P)].bitcast(FP4X4)
+
+        order_w1(0, 1, "w1_c")
         w3_c = held("w3_c", [P, PASSES * H], I32)
         reorder_columns(w3_c[:], w3_raw[:])
-        w_s = held("w_s", [P, PASSES * H], U8)
-        reorder_columns(w_s[:], w_s_raw[:])
+        w1_s = held("w1_s", [P, PASSES * H], U8)
+        reorder_columns(w1_s[:], w1_s_raw[:])
+        w3_s = held("w3_s", [P, PASSES * H], U8)
+        reorder_columns(w3_s[:], w3_s_raw[:])
 
         w2_rounded = [held("w2_rounded%d" % g, [P, PACK * H], BF16) for g in range(PASSES)]
-        w2_c = [held("w2_c%d" % g, [P, H], I32) for g in range(PASSES)]
         w2_s = [held("w2_s%d" % g, [P, H], U8) for g in range(PASSES)]
+        w2_c = []
         for g in range(PASSES):
-            nc.scalar.copy(
-                w2_rounded[g][:].rearrange("p (t m i) -> p m i t", t=PACK, i=PACK),
-                w2_raw[g][:].rearrange("p i (m t) -> p m i t", t=PACK),
-            )
-            nc.vector.quantize_mx(w2_c[g][:].bitcast(FP8X4), w2_s[g][:], w2_rounded[g][:])
+            ordered = w2_rounded[g][:].rearrange("p (t m i) -> p m i t", t=PACK, i=PACK)
+            raw = w2_raw[g][:].rearrange("p i (m t) -> p m i t", t=PACK)
+            if g == 0:
+                nc.scalar.copy(ordered, raw)
+                codes = held("w2_c0", [P, H], I32)
+                nc.vector.quantize_mx(codes[:].bitcast(FP8X4), w2_s[g][:], w2_rounded[g][:])
+                w2_c.append([codes[:, span(t, P)] for t in range(PACK)])
+                continue
+            nc.vector.tensor_copy(ordered[:, :, :, 0:2], raw[:, :, :, 0:2])
+            nc.scalar.copy(ordered[:, :, :, 2:4], raw[:, :, :, 2:4])
+            w2_c.append([])
+            for u, tag in enumerate(("w2_c1", "w3_raw")):
+                codes = held("w2_c1", [P, H // 2], I32, tag)
+                nc.vector.quantize_mx(
+                    codes[:].bitcast(FP8X4), w2_s[g][:, span(u, H // 2)], w2_rounded[g][:, span(u, PACK * H // 2)]
+                )
+                w2_c[g].extend(codes[:, span(t, P)] for t in range(2))
 
         page_rounded = [held("page_rounded%d" % c, [P, N, PACK], BF16) for c in range(CHUNKS)]
-        w1_bytes = w1_c[:].bitcast(U8)
 
-        def product(tag, half, codes, scales, v_scales):
-            acc = bank(tag)
+        def product(banks, piece, codes, scales, v_scales):
+            half = piece % HALVES
+            acc = bank(banks[piece % len(banks)])
             for g in range(PASSES):
                 nc.tensor.matmul_mx(
                     acc[:], lhsT=codes[g], lhsT_scale=scales[g], rhs=v_w[g][half][:].bitcast(FP8X4),
@@ -176,34 +203,39 @@ def tile_list_tow_dispatch_scores_kernel(
             return acc
 
         def refill(t, half):
+            piece = HALVES * t + half
             blocks = [PACK * g + t for g in range(PASSES)]
             acc_a = product(
-                "a", half, [w1_bytes[:, span(b, 2 * P)].bitcast(FP4X4) for b in blocks],
-                [w_s[:, span(b, P)] for b in blocks], v_s_from_row0,
+                BANKS["a"], piece, [w1_slice(t, g) for g in range(PASSES)],
+                [w1_s[:, span(b, P)] for b in blocks], v_s_from_row0,
             )
-            a_sb = ring.tile([P, N], F32, name="a_sb", tag="a_then_x")
+            if piece == 0:
+                a_sb = held("a_sb", [P, N], F32, "a_then_w1")
+            else:
+                a_sb = ring.tile([P, N], F32, name="a_sb", tag="a_then_x")
             nc.scalar.copy(a_sb[:], acc_a[:])
             acc_b = product(
-                "b", half, [w2_c[g][:, span(t, P)].bitcast(FP8X4) for g in range(PASSES)],
+                BANKS["b"], piece, [w2_c[g][t].bitcast(FP8X4) for g in range(PASSES)],
                 [w2_s[g][:, span(t, P)] for g in range(PASSES)], v_s,
             )
             acc_c = product(
-                "c", half, [w3_c[:, span(b, P)].bitcast(FP8X4) for b in blocks],
-                [w_s[4:, span(b, P)] for b in blocks], v_s,
+                BANKS["c"], piece, [w3_c[:, span(b, P)].bitcast(FP8X4) for b in blocks],
+                [w3_s[:, span(b, P)] for b in blocks], v_s,
             )
-            first_piece = t == 0 and half == 0
-            if not first_piece:
-                c_sb = ring.tile([P, N], F32, name="c_sb")
-                nc.scalar.copy(c_sb[:], acc_c[:])
             weights = gain[t][:, span(half, N)]
-            fill = ring.tile([P, N], F32, name="fill", bufs=FILL_BUFS)
-            nc.vector.tensor_tensor(fill[:], acc_b[:], a_sb[:], ALU.min)
-            if first_piece:
+            fill = keep.tile([P, N], F32, name="fill", tag="c_then_fill%d" % (piece - 1 if piece > 1 else PIECES + piece))
+            if piece == 0:
+                nc.vector.tensor_tensor(fill[:], acc_b[:], a_sb[:], ALU.min)
                 nc.vector.tensor_tensor(fill[:], acc_c[:], fill[:], ALU.mult)
                 nc.vector.tensor_tensor(fill[:], fill[:], weights, ALU.mult)
+                order_w1(1, PACK - 1, "a_then_w1")
             else:
-                nc.gpsimd.tensor_tensor(c_sb[:], c_sb[:], weights, ALU.mult)
-                nc.gpsimd.tensor_tensor(fill[:], fill[:], c_sb[:], ALU.mult)
+                c_sb = keep.tile([P, N], F32, name="c_sb", tag="c_then_fill%d" % piece)
+                nc.scalar.copy(c_sb[:], acc_c[:])
+                weighted = ring.tile([P, N], F32, name="weighted", bufs=2)
+                nc.gpsimd.tensor_tensor(weighted[:], c_sb[:], weights, ALU.mult)
+                nc.vector.tensor_tensor(fill[:], acc_b[:], a_sb[:], ALU.min)
+                nc.gpsimd.tensor_tensor(fill[:], fill[:], weighted[:], ALU.mult)
             nc.vector.tensor_copy(page[t][:].indirect(list3[:, span(half, LIST_COLS)]), fill[:])
 
         def round_slice(t):
@@ -236,7 +268,7 @@ def tile_list_tow_dispatch_scores_kernel(
         picked = []
         for n in range(GROUPS):
             for c in range(CHUNKS):
-                acc_e = bank("a")
+                acc_e = bank(c)
                 nc.tensor.matmul_mx(
                     acc_e[:], lhsT=v2_w[:, span(n, P)].bitcast(FP8X4), lhsT_scale=v2_s[:, span(n, P)],
                     rhs=page_c[c][:].bitcast(FP8X4), rhs_scale=page_s[c][:], start=True, stop=True,

@@ -27,6 +27,7 @@ QUADRANTS = 4
 LIST_COLS = N // 16
 
 PIECES = PACK * HALVES
+DIFFERENCE_PIECES = (3, 5, 7)
 BANKS = {"a": (0, 1), "b": (2, 3, 4), "c": (5, 6, 7)}
 VECTOR_CHUNKS = 2
 FIRST_SQUARES = {"gpsimd": 6, "scalar": 0}
@@ -59,13 +60,10 @@ def tile_list_tow_dispatch_scores_kernel(
 
         tab_s = held("tab_s", [P, T], U8)
         v_s1 = held("v_s1", [P, S], U8)
-        w1_s_raw = held("w1_s_raw", [P, PASSES * H], U8)
-        w3_s_raw = held("w3_s_raw", [P, PASSES * H], U8)
+        w_s_raw = held("w_s_raw", [P, PASSES * H], U8)
         tab2_s = held("tab2_s", [P, T3], U8)
-        nc.vector.memset(tab_s[:, span(0, T // 2)].bitcast(I32), 0)
-        nc.gpsimd.memset(tab_s[:, span(1, T // 2)].bitcast(I32), 0)
-        nc.gpsimd.memset(tab2_s[:].bitcast(I32), 0)
-        for scales in (w1_s_raw, w3_s_raw, v_s1):
+        nc.gpsimd.memset(tab_s[:].bitcast(I32), 0)
+        for scales in (tab2_s, w_s_raw, v_s1):
             nc.vector.memset(scales[:].bitcast(I32), 0)
 
         tab_w = [held("tab_w%d" % g, [P, T], I32) for g in range(PASSES)]
@@ -73,7 +71,7 @@ def tile_list_tow_dispatch_scores_kernel(
         avail_sb = held("avail_sb", [P, GROUPS], F32)
         w2_raw = [held("w2_raw%d" % g, [P, PACK, H], F32) for g in range(PASSES)]
         w3_raw = held("w3_raw", [P, PASSES * H], I32)
-        gain = [held("gain%d" % t, [P, S], F32) for t in range(PACK)]
+        gain = [held("gain%d" % piece, [P, N], F32) for piece in range(PIECES)]
         page = [held("page%d" % t, [P, T2], F32) for t in range(PACK)]
         tab2_w = held("tab2_w", [P, T3], I32)
 
@@ -83,25 +81,30 @@ def tile_list_tow_dispatch_scores_kernel(
         def load_w2(g):
             nc.sync.dma_start(w2_raw[g][:], w2[span(g, P * PACK), :].rearrange("(p i) r -> p i r", i=PACK))
 
-        def load_weight_scales(tile, scales):
-            rows = tile[:].bitcast(I32).rearrange("p (g r) -> p g r", g=PASSES)
-            for q in range(QUADRANTS):
+        def load_weight_scales(scales, first, quadrants):
+            rows = w_s_raw[:].bitcast(I32).rearrange("p (g r) -> p g r", g=PASSES)
+            for q in quadrants:
                 source = scales[:, span(q, 4), :].rearrange("g b r -> b g r")
-                nc.sync.dma_start(rows[32 * q : 32 * q + 4], source.bitcast(I32))
+                nc.sync.dma_start(rows[32 * q + first : 32 * q + first + 4], source.bitcast(I32))
 
         def load_gain(t, half):
             rows = wgs.rearrange("(m t) j -> m t j", t=PACK)
             for q in (0, 2, 1, 3):
-                nc.sync.dma_start(gain[t][span(q, 32), span(half, N)], rows[:, t, span(half, N)])
+                nc.sync.dma_start(gain[HALVES * t + half][span(q, 32), :], rows[:, t, span(half, N)])
 
         nc.sync.dma_start(list1[:], offs)
+        nc.sync.dma_start(list2[:], offs2)
         with nc.allow_non_contiguous_dma(reason="one availability weight to a partition and group"):
             nc.scalar.dma_start(avail_sb[:], avail.rearrange("(n p) -> p n", p=P))
         for q in range(QUADRANTS):
             nc.sync.dma_start(tab_s[32 * q : 32 * q + 8, :].bitcast(I32), tab_scales[:, span(q, 4), :].bitcast(I32))
         load_words(tab_w[0], tab_words[0])
+        for q in range(QUADRANTS):
+            nc.sync.dma_start(tab2_s[32 * q : 32 * q + 4, :].bitcast(I32), tab2_scales[0, span(q, 4), :].bitcast(I32))
+        load_weight_scales(w1_scales, 0, (0, 1))
         load_words(tab_w[1], tab_words[1])
-        load_weight_scales(w1_s_raw, w1_scales)
+        load_weight_scales(w1_scales, 0, (2, 3))
+        load_weight_scales(w3_scales, 4, range(QUADRANTS))
         load_w2(0)
         nc.sync.dma_start(
             w1_raw[:].rearrange("p (g r) -> p g r", g=PASSES), w1_words.rearrange("g p r -> p g r").bitcast(I32)
@@ -109,7 +112,6 @@ def tile_list_tow_dispatch_scores_kernel(
         v_s0 = held("v_s0", [P, S], U8)
         nc.vector.tensor_copy(v_s0[:], tab_s[:].indirect(list1[:]))
         nc.sync.dma_start(v_s1[0:112, :].bitcast(I32), v_s0[4:116, :].bitcast(I32))
-        load_weight_scales(w3_s_raw, w3_scales)
         load_w2(1)
         nc.sync.dma_start(
             w3_raw[:].rearrange("p (g r) -> p g r", g=PASSES), w3_words.rearrange("g p r i -> p g (r i)").bitcast(I32)
@@ -120,10 +122,6 @@ def tile_list_tow_dispatch_scores_kernel(
             load_gain(t, 0)
             nc.sync.dma_start(page[t][:], page_rows[:, t, :])
             if t == PACK - 1:
-                nc.sync.dma_start(list2[:], offs2)
-                for q in range(QUADRANTS):
-                    rows = tab2_scales[0, span(q, 4), :]
-                    nc.sync.dma_start(tab2_s[32 * q : 32 * q + 4, :].bitcast(I32), rows.bitcast(I32))
                 load_words(tab2_w, tab2_words[0])
             load_gain(t, 1)
         nc.sync.dma_start(list4[:], offs4)
@@ -141,19 +139,19 @@ def tile_list_tow_dispatch_scores_kernel(
                 window = tab_w[g][:].bitcast(U32)
                 nc.vector.tensor_copy(v_w[g][half][:].bitcast(U32), window.indirect(list1[:, span(half, LIST_COLS)]))
 
-        def reorder_columns(ordered, raw):
+        def reorder_columns(ordered, raw, run):
             nc.vector.tensor_copy(
-                ordered.rearrange("p (g t m) -> p g m t", g=PASSES, t=PACK),
-                raw.rearrange("p (g m t) -> p g m t", g=PASSES, t=PACK),
+                ordered.rearrange("p (g t m j) -> p g m t j", g=PASSES, t=PACK, j=run),
+                raw.rearrange("p (g m j t) -> p g m t j", g=PASSES, t=PACK, j=run),
             )
 
-        w1_cols = w1_raw[:].bitcast(U16).rearrange("p (g m t) -> p g m t", g=PASSES, t=PACK)
+        w1_cols = w1_raw[:].bitcast(U16).rearrange("p (g m j t) -> p g m t j", g=PASSES, t=PACK, j=8)
         w1_c = {}
 
         def order_w1(first, count, tag):
             tile = held("w1_c", [P, count * PASSES * P // 2], I32, tag)
-            ordered = tile[:].bitcast(U16).rearrange("p (t g m) -> p g m t", g=PASSES, t=count)
-            nc.vector.tensor_copy(ordered, w1_cols[:, :, :, first : first + count])
+            ordered = tile[:].bitcast(U16).rearrange("p (t g m j) -> p g m t j", g=PASSES, t=count, j=8)
+            nc.vector.tensor_copy(ordered, w1_cols[:, :, :, first : first + count, :])
             for t in range(count):
                 w1_c[first + t] = tile[:].bitcast(U8)[:, span(t, PASSES * 2 * P)]
 
@@ -162,26 +160,24 @@ def tile_list_tow_dispatch_scores_kernel(
 
         order_w1(0, 1, "w1_c")
         w3_c = held("w3_c", [P, PASSES * H], I32)
-        reorder_columns(w3_c[:], w3_raw[:])
-        w1_s = held("w1_s", [P, PASSES * H], U8)
-        reorder_columns(w1_s[:], w1_s_raw[:])
-        w3_s = held("w3_s", [P, PASSES * H], U8)
-        reorder_columns(w3_s[:], w3_s_raw[:])
+        reorder_columns(w3_c[:], w3_raw[:], 4)
+        w_s = held("w_s", [P, PASSES * H], U8)
+        reorder_columns(w_s[:], w_s_raw[:], 16)
 
         w2_rounded = [held("w2_rounded%d" % g, [P, PACK * H], BF16) for g in range(PASSES)]
         w2_s = [held("w2_s%d" % g, [P, H], U8) for g in range(PASSES)]
         w2_c = []
         for g in range(PASSES):
-            ordered = w2_rounded[g][:].rearrange("p (t m i) -> p m i t", t=PACK, i=PACK)
-            raw = w2_raw[g][:].rearrange("p i (m t) -> p m i t", t=PACK)
+            ordered = w2_rounded[g][:].rearrange("p (t m i) -> p m t i", t=PACK, i=PACK)
+            raw = w2_raw[g][:].rearrange("p i (m t) -> p m t i", t=PACK)
             if g == 0:
-                nc.scalar.copy(ordered, raw)
+                nc.scalar.mul(ordered, raw, -1.0)
                 codes = held("w2_c0", [P, H], I32)
                 nc.vector.quantize_mx(codes[:].bitcast(FP8X4), w2_s[g][:], w2_rounded[g][:])
                 w2_c.append([codes[:, span(t, P)] for t in range(PACK)])
                 continue
-            nc.vector.tensor_copy(ordered[:, :, :, 0:2], raw[:, :, :, 0:2])
-            nc.scalar.copy(ordered[:, :, :, 2:4], raw[:, :, :, 2:4])
+            nc.vector.tensor_scalar(ordered[:, :, 0:2], raw[:, :, 0:2], -1.0, None, ALU.mult)
+            nc.scalar.mul(ordered[:, :, 2:4], raw[:, :, 2:4], -1.0)
             w2_c.append([])
             for u, tag in enumerate(("w2_c1", "w3_raw")):
                 codes = held("w2_c1", [P, H // 2], I32, tag)
@@ -192,61 +188,76 @@ def tile_list_tow_dispatch_scores_kernel(
 
         page_rounded = [held("page_rounded%d" % c, [P, N, PACK], BF16) for c in range(CHUNKS)]
 
-        def product(banks, piece, codes, scales, v_scales):
+        def product(banks, piece, passes):
             half = piece % HALVES
             acc = bank(banks[piece % len(banks)])
-            for g in range(PASSES):
+            for i, (codes, scales, g, v_scales) in enumerate(passes):
                 nc.tensor.matmul_mx(
-                    acc[:], lhsT=codes[g], lhsT_scale=scales[g], rhs=v_w[g][half][:].bitcast(FP8X4),
-                    rhs_scale=v_scales[g][:, span(half, N)], start=g == 0, stop=g == PASSES - 1,
+                    acc[:], lhsT=codes, lhsT_scale=scales, rhs=v_w[g][half][:].bitcast(FP8X4),
+                    rhs_scale=v_scales[g][:, span(half, N)], start=i == 0, stop=i == len(passes) - 1,
                 )
             return acc
 
         def refill(t, half):
             piece = HALVES * t + half
+            by_difference = piece in DIFFERENCE_PIECES
             blocks = [PACK * g + t for g in range(PASSES)]
-            acc_a = product(
-                BANKS["a"], piece, [w1_slice(t, g) for g in range(PASSES)],
-                [w1_s[:, span(b, P)] for b in blocks], v_s_from_row0,
-            )
+            passes_a = [(w1_slice(t, g), w_s[:, span(blocks[g], P)], g, v_s_from_row0) for g in range(PASSES)]
+            passes_b = [(w2_c[g][t].bitcast(FP8X4), w2_s[g][:, span(t, P)], g, v_s) for g in range(PASSES)]
+            passes_c = [
+                (w3_c[:, span(blocks[g], P)].bitcast(FP8X4), w_s[4:, span(blocks[g], P)], g, v_s) for g in range(PASSES)
+            ]
+            acc_a = product(BANKS["a"], piece, passes_a)
             if piece == 0:
                 a_sb = held("a_sb", [P, N], F32, "a_then_w1")
             else:
                 a_sb = ring.tile([P, N], F32, name="a_sb", tag="a_then_x")
             nc.scalar.copy(a_sb[:], acc_a[:])
-            acc_b = product(
-                BANKS["b"], piece, [w2_c[g][t].bitcast(FP8X4) for g in range(PASSES)],
-                [w2_s[g][:, span(t, P)] for g in range(PASSES)], v_s,
-            )
-            acc_c = product(
-                BANKS["c"], piece, [w3_c[:, span(b, P)].bitcast(FP8X4) for b in blocks],
-                [w3_s[:, span(b, P)] for b in blocks], v_s,
-            )
-            weights = gain[t][:, span(half, N)]
+            if not by_difference:
+                acc_b = product(BANKS["b"], piece, passes_b)
+            else:
+                acc_b = product(BANKS["a"][::-1], piece, passes_a + passes_b)
+                excess = ring.tile([P, N], F32, name="excess", bufs=len(DIFFERENCE_PIECES))
+                nc.scalar.activation(excess[:], acc_b[:], ACT.Relu)
+            acc_c = product(BANKS["c"], piece, passes_c)
+            weights = gain[piece][:]
             fill = keep.tile([P, N], F32, name="fill", tag="c_then_fill%d" % (piece - 1 if piece > 1 else PIECES + piece))
+            if piece > 0:
+                c_sb = keep.tile([P, N], F32, name="c_sb", tag="c_then_fill%d" % piece)
+                nc.scalar.copy(c_sb[:], acc_c[:])
+                weighted = held("weighted", [P, N], F32, "gain%d" % (piece - 1))
+                nc.gpsimd.tensor_tensor(weighted[:], c_sb[:], weights, ALU.mult)
+            if by_difference:
+                nc.gpsimd.tensor_tensor(fill[:], a_sb[:], excess[:], ALU.subtract)
+            else:
+                nc.vector.scalar_tensor_tensor(fill[:], acc_b[:], -1.0, a_sb[:], ALU.mult, ALU.min)
             if piece == 0:
-                nc.vector.tensor_tensor(fill[:], acc_b[:], a_sb[:], ALU.min)
                 nc.vector.tensor_tensor(fill[:], acc_c[:], fill[:], ALU.mult)
                 nc.vector.tensor_tensor(fill[:], fill[:], weights, ALU.mult)
                 order_w1(1, PACK - 1, "a_then_w1")
             else:
-                c_sb = keep.tile([P, N], F32, name="c_sb", tag="c_then_fill%d" % piece)
-                nc.scalar.copy(c_sb[:], acc_c[:])
-                weighted = ring.tile([P, N], F32, name="weighted", bufs=2)
-                nc.gpsimd.tensor_tensor(weighted[:], c_sb[:], weights, ALU.mult)
-                nc.vector.tensor_tensor(fill[:], acc_b[:], a_sb[:], ALU.min)
                 nc.gpsimd.tensor_tensor(fill[:], fill[:], weighted[:], ALU.mult)
             nc.vector.tensor_copy(page[t][:].indirect(list3[:, span(half, LIST_COLS)]), fill[:])
+
+        pairs = [held("pairs", [P, 2, N, 2], BF16, "w2_raw%d" % c) for c in range(VECTOR_CHUNKS)]
 
         def round_slice(t):
             for c in range(CHUNKS):
                 source = page[t][:, span(c, N)]
-                if t == PACK - 2 and c < VECTOR_CHUNKS:
-                    nc.scalar.copy(page_rounded[c][:, :, t : t + 2], source.unsqueeze(2).to_broadcast([P, N, 2]))
-                elif t == PACK - 1 and c < VECTOR_CHUNKS:
-                    nc.vector.tensor_copy(page_rounded[c][:, :, t], source)
-                else:
+                if c >= VECTOR_CHUNKS:
                     nc.scalar.copy(page_rounded[c][:, :, t], source)
+                elif t < PACK - 2:
+                    nc.scalar.copy(pairs[c][:, 0, :, t], source)
+                elif t == PACK - 2:
+                    nc.scalar.copy(pairs[c][:, 1], source.unsqueeze(2).to_broadcast([P, N, 2]))
+                else:
+                    nc.vector.tensor_copy(pairs[c][:, 1, :, 1], source)
+            if t == PACK - 1:
+                for c in range(VECTOR_CHUNKS):
+                    nc.vector.tensor_copy(
+                        page_rounded[c][:].rearrange("p n t -> p (n t)").bitcast(I32).rearrange("p (n u) -> p n u", u=2),
+                        pairs[c][:].rearrange("p u n e -> p (u n e)").bitcast(I32).rearrange("p (u n) -> p n u", u=2),
+                    )
 
         v2_w = held("v2_w", [P, S2], I32)
         v2_s = held("v2_s", [P, S2], U8)

@@ -1,6 +1,7 @@
 from contextlib import ExitStack
 
 import concourse.mybir as mybir
+from concourse.masks import make_identity
 
 K, T, S, H, T2, T3, S2, PICKED = 1024, 2048, 1024, 512, 2048, 2048, 512, 1024
 FLOPS = 2 * (3 * K * H * S + H * S2 * T2)
@@ -24,6 +25,7 @@ HALVES = S // N
 CHUNKS = T2 // N
 GROUPS = S2 // P
 QUADRANTS = 4
+PORT_ORDER = (0, 2, 1, 3)
 LIST_COLS = N // 16
 
 PIECES = PACK * HALVES
@@ -62,13 +64,17 @@ def tile_list_tow_dispatch_scores_kernel(
         v_s1 = held("v_s1", [P, S], U8)
         w_s_raw = held("w_s_raw", [P, PASSES * H], U8)
         tab2_s = held("tab2_s", [P, T3], U8)
+        avail_rows = held("avail_rows", [P, P], F32)
+        identity = held("identity", [P, P], F32)
         nc.gpsimd.memset(tab_s[:].bitcast(I32), 0)
-        for scales in (tab2_s, w_s_raw, v_s1):
+        nc.gpsimd.memset(avail_rows[:], 0.0)
+        make_identity(nc, identity[:])
+        nc.gpsimd.memset(tab2_s[:].bitcast(I32), 0)
+        for scales in (w_s_raw, v_s1):
             nc.vector.memset(scales[:].bitcast(I32), 0)
 
         tab_w = [held("tab_w%d" % g, [P, T], I32) for g in range(PASSES)]
         w1_raw = held("w1_raw", [P, PASSES * H // 2], I32)
-        avail_sb = held("avail_sb", [P, GROUPS], F32)
         w2_raw = [held("w2_raw%d" % g, [P, PACK, H], F32) for g in range(PASSES)]
         w3_raw = held("w3_raw", [P, PASSES * H], I32)
         gain = [held("gain%d" % piece, [P, N], F32) for piece in range(PIECES)]
@@ -89,26 +95,25 @@ def tile_list_tow_dispatch_scores_kernel(
 
         def load_gain(t, half):
             rows = wgs.rearrange("(m t) j -> m t j", t=PACK)
-            for q in (0, 2, 1, 3):
+            for q in PORT_ORDER:
                 nc.sync.dma_start(gain[HALVES * t + half][span(q, 32), :], rows[:, t, span(half, N)])
 
         nc.sync.dma_start(list1[:], offs)
-        nc.sync.dma_start(list2[:], offs2)
-        with nc.allow_non_contiguous_dma(reason="one availability weight to a partition and group"):
-            nc.scalar.dma_start(avail_sb[:], avail.rearrange("(n p) -> p n", p=P))
+        nc.sync.dma_start(list3[:], offs3)
+        nc.scalar.dma_start(avail_rows[0:GROUPS, :], avail.rearrange("(n p) -> n p", p=P))
         for q in range(QUADRANTS):
             nc.sync.dma_start(tab_s[32 * q : 32 * q + 8, :].bitcast(I32), tab_scales[:, span(q, 4), :].bitcast(I32))
         load_words(tab_w[0], tab_words[0])
-        for q in range(QUADRANTS):
-            nc.sync.dma_start(tab2_s[32 * q : 32 * q + 4, :].bitcast(I32), tab2_scales[0, span(q, 4), :].bitcast(I32))
-        load_weight_scales(w1_scales, 0, (0, 1))
+        for q in PORT_ORDER:
+            nc.gpsimd.dma_start(tab2_s[32 * q : 32 * q + 4, :].bitcast(I32), tab2_scales[0, span(q, 4), :].bitcast(I32))
+        load_weight_scales(w1_scales, 0, PORT_ORDER)
         load_words(tab_w[1], tab_words[1])
-        load_weight_scales(w1_scales, 0, (2, 3))
-        load_weight_scales(w3_scales, 4, range(QUADRANTS))
+        load_weight_scales(w3_scales, 4, PORT_ORDER)
         load_w2(0)
         nc.sync.dma_start(
             w1_raw[:].rearrange("p (g r) -> p g r", g=PASSES), w1_words.rearrange("g p r -> p g r").bitcast(I32)
         )
+        nc.sync.dma_start(list2[:], offs2)
         v_s0 = held("v_s0", [P, S], U8)
         nc.vector.tensor_copy(v_s0[:], tab_s[:].indirect(list1[:]))
         nc.sync.dma_start(v_s1[0:112, :].bitcast(I32), v_s0[4:116, :].bitcast(I32))
@@ -116,7 +121,6 @@ def tile_list_tow_dispatch_scores_kernel(
         nc.sync.dma_start(
             w3_raw[:].rearrange("p (g r) -> p g r", g=PASSES), w3_words.rearrange("g p r i -> p g (r i)").bitcast(I32)
         )
-        nc.sync.dma_start(list3[:], offs3)
         page_rows = page0.rearrange("(p t) c -> p t c", t=PACK)
         for t in range(PACK):
             load_gain(t, 0)
@@ -128,7 +132,9 @@ def tile_list_tow_dispatch_scores_kernel(
 
         root = held("root", [P, GROUPS], F32)
         inv_avail = held("inv_avail", [P, GROUPS], F32)
-        nc.scalar.activation(root[:], avail_sb[:], ACT.Abs_reciprocal_sqrt)
+        avail_cols = bank(BANKS["c"][-1])
+        nc.tensor.transpose(avail_cols[:, 0:P], avail_rows[:], identity[:])
+        nc.scalar.activation(root[:], avail_cols[:, 0:GROUPS], ACT.Abs_reciprocal_sqrt)
         nc.scalar.activation(inv_avail[:], root[:], ACT.Square)
 
         v_s = [v_s0[:], v_s0[4:]]

@@ -30,10 +30,16 @@ LIST_COLS = N // 16
 
 PIECES = PACK * HALVES
 DIFFERENCE_PIECES = (3, 5, 7)
-BANKS = {"a": (0, 1), "b": (2, 3, 4), "c": (5, 6, 7)}
 VECTOR_CHUNKS = 2
-FIRST_SQUARES = {"gpsimd": 6, "scalar": 0}
-SECOND_SQUARES = {"gpsimd": 0, "scalar": 4}
+PAIR_CHUNK = 1
+GPSIMD_FIRST_SQUARES = range(6)
+SCALAR_SECOND_SQUARES = (0,1,2,3,7)
+VECTOR_COPIES = ((1, 0), (0, 3))
+BANKS = 8
+EARLY_PIECES = 3
+EARLY_BANKS = ((0, 1, 2, 3), (4, 5, 4, 6))
+LATE_BANKS = (3, 4, 6)
+FIRST_BANKS = {"a then c": (0, 1, 2), "c then a": (3, 4), "b": (5, 6, 7)}
 
 
 def tile_list_tow_dispatch_scores_kernel(
@@ -61,16 +67,18 @@ def tile_list_tow_dispatch_scores_kernel(
         list4 = held("list4", [P, PICKED // 16], U16)
 
         tab_s = held("tab_s", [P, T], U8)
-        v_s1 = held("v_s1", [P, S], U8)
-        w_s_raw = held("w_s_raw", [P, PASSES * H], U8)
         tab2_s = held("tab2_s", [P, T3], U8)
+        v_s = held("v_s", [P, PASSES * S], U8)
+        v2_s = held("v2_s", [P, S2], U8)
+        w1_s_raw = held("w1_s_raw", [P, PASSES * H], U8)
+        w3_s_raw = held("w3_s_raw", [P, PASSES * H], U8)
         avail_rows = held("avail_rows", [P, P], F32)
         identity = held("identity", [P, P], F32)
         nc.gpsimd.memset(tab_s[:].bitcast(I32), 0)
         nc.gpsimd.memset(avail_rows[:], 0.0)
         make_identity(nc, identity[:])
         nc.gpsimd.memset(tab2_s[:].bitcast(I32), 0)
-        for scales in (w_s_raw, v_s1):
+        for scales in (w1_s_raw, v_s, w3_s_raw, v2_s):
             nc.vector.memset(scales[:].bitcast(I32), 0)
 
         tab_w = [held("tab_w%d" % g, [P, T], I32) for g in range(PASSES)]
@@ -87,36 +95,39 @@ def tile_list_tow_dispatch_scores_kernel(
         def load_w2(g):
             nc.sync.dma_start(w2_raw[g][:], w2[span(g, P * PACK), :].rearrange("(p i) r -> p i r", i=PACK))
 
-        def load_weight_scales(scales, first, quadrants):
-            rows = w_s_raw[:].bitcast(I32).rearrange("p (g r) -> p g r", g=PASSES)
-            for q in quadrants:
+        def load_weight_scales(planes, scales):
+            rows = planes[:].bitcast(I32).rearrange("p (g r) -> p g r", g=PASSES)
+            for q in PORT_ORDER:
                 source = scales[:, span(q, 4), :].rearrange("g b r -> b g r")
-                nc.sync.dma_start(rows[32 * q + first : 32 * q + first + 4], source.bitcast(I32))
+                nc.sync.dma_start(rows[32 * q : 32 * q + 4], source.bitcast(I32))
 
         def load_gain(t, half):
             rows = wgs.rearrange("(m t) j -> m t j", t=PACK)
             for q in PORT_ORDER:
                 nc.sync.dma_start(gain[HALVES * t + half][span(q, 32), :], rows[:, t, span(half, N)])
 
+        def spread_scale_rows(planes, rows, passes):
+            for q in PORT_ORDER:
+                target = planes[32 * q : 32 * q + 4, :].bitcast(I32).rearrange("p (g j) -> p g j", g=passes)
+                nc.sync.dma_start(target, rows[span(q, 4 * passes), :].bitcast(I32))
+
         nc.sync.dma_start(list1[:], offs)
         nc.sync.dma_start(list3[:], offs3)
         nc.scalar.dma_start(avail_rows[0:GROUPS, :], avail.rearrange("(n p) -> n p", p=P))
-        for q in range(QUADRANTS):
-            nc.sync.dma_start(tab_s[32 * q : 32 * q + 8, :].bitcast(I32), tab_scales[:, span(q, 4), :].bitcast(I32))
+        nc.sync.dma_start(tab_s[0:32, :].bitcast(I32), tab_scales.rearrange("g q t -> q g t").bitcast(I32))
         load_words(tab_w[0], tab_words[0])
-        for q in PORT_ORDER:
-            nc.gpsimd.dma_start(tab2_s[32 * q : 32 * q + 4, :].bitcast(I32), tab2_scales[0, span(q, 4), :].bitcast(I32))
-        load_weight_scales(w1_scales, 0, PORT_ORDER)
+        nc.gpsimd.dma_start(tab2_s[0:16, :].bitcast(I32), tab2_scales[0].bitcast(I32))
+        load_weight_scales(w1_s_raw, w1_scales)
         load_words(tab_w[1], tab_words[1])
-        load_weight_scales(w3_scales, 4, PORT_ORDER)
-        load_w2(0)
+        nc.sync.dma_start(list2[:], offs2)
+        v_rows = held("v_rows", [P, S], U8)
+        nc.vector.tensor_copy(v_rows[:], tab_s[:].indirect(list1[:]))
+        spread_scale_rows(v_s, v_rows, PASSES)
         nc.sync.dma_start(
             w1_raw[:].rearrange("p (g r) -> p g r", g=PASSES), w1_words.rearrange("g p r -> p g r").bitcast(I32)
         )
-        nc.sync.dma_start(list2[:], offs2)
-        v_s0 = held("v_s0", [P, S], U8)
-        nc.vector.tensor_copy(v_s0[:], tab_s[:].indirect(list1[:]))
-        nc.sync.dma_start(v_s1[0:112, :].bitcast(I32), v_s0[4:116, :].bitcast(I32))
+        load_w2(0)
+        load_weight_scales(w3_s_raw, w3_scales)
         load_w2(1)
         nc.sync.dma_start(
             w3_raw[:].rearrange("p (g r) -> p g r", g=PASSES), w3_words.rearrange("g p r i -> p g (r i)").bitcast(I32)
@@ -132,13 +143,11 @@ def tile_list_tow_dispatch_scores_kernel(
 
         root = held("root", [P, GROUPS], F32)
         inv_avail = held("inv_avail", [P, GROUPS], F32)
-        avail_cols = bank(BANKS["c"][-1])
+        avail_cols = bank(BANKS - 1)
         nc.tensor.transpose(avail_cols[:, 0:P], avail_rows[:], identity[:])
         nc.scalar.activation(root[:], avail_cols[:, 0:GROUPS], ACT.Abs_reciprocal_sqrt)
         nc.scalar.activation(inv_avail[:], root[:], ACT.Square)
 
-        v_s = [v_s0[:], v_s0[4:]]
-        v_s_from_row0 = [v_s0[:], v_s1[:]]
         v_w = [[held("v_w%d_%d" % (g, half), [P, N], I32) for half in range(HALVES)] for g in range(PASSES)]
         for g in range(PASSES):
             for half in range(HALVES):
@@ -151,168 +160,186 @@ def tile_list_tow_dispatch_scores_kernel(
                 raw.rearrange("p (g m j t) -> p g m t j", g=PASSES, t=PACK, j=run),
             )
 
-        w1_cols = w1_raw[:].bitcast(U16).rearrange("p (g m j t) -> p g m t j", g=PASSES, t=PACK, j=8)
-        w1_c = {}
-
-        def order_w1(first, count, tag):
-            tile = held("w1_c", [P, count * PASSES * P // 2], I32, tag)
-            ordered = tile[:].bitcast(U16).rearrange("p (t g m j) -> p g m t j", g=PASSES, t=count, j=8)
-            nc.vector.tensor_copy(ordered, w1_cols[:, :, :, first : first + count, :])
-            for t in range(count):
-                w1_c[first + t] = tile[:].bitcast(U8)[:, span(t, PASSES * 2 * P)]
-
-        def w1_slice(t, g):
-            return w1_c[t][:, span(g, 2 * P)].bitcast(FP4X4)
-
-        order_w1(0, 1, "w1_c")
-        w3_c = held("w3_c", [P, PASSES * H], I32)
-        reorder_columns(w3_c[:], w3_raw[:], 4)
-        w_s = held("w_s", [P, PASSES * H], U8)
-        reorder_columns(w_s[:], w_s_raw[:], 16)
+        w1_c = held("w1_c", [P, PASSES * H // 2], I32)
+        reorder_columns(w1_c[:].bitcast(U16), w1_raw[:].bitcast(U16), 8)
+        v2_rows = held("v2_rows", [P, S2], U8, "w1_raw")
+        nc.vector.tensor_copy(v2_rows[:], tab2_s[:].indirect(list2[:]))
+        spread_scale_rows(v2_s, v2_rows, 1)
+        w1_s = held("w1_s", [P, PASSES * H], U8)
+        reorder_columns(w1_s[:], w1_s_raw[:], 16)
 
         w2_rounded = [held("w2_rounded%d" % g, [P, PACK * H], BF16) for g in range(PASSES)]
         w2_s = [held("w2_s%d" % g, [P, H], U8) for g in range(PASSES)]
-        w2_c = []
-        for g in range(PASSES):
+        w2_c = {}
+
+        def round_w2(g):
             ordered = w2_rounded[g][:].rearrange("p (t m i) -> p m t i", t=PACK, i=PACK)
             raw = w2_raw[g][:].rearrange("p i (m t) -> p m t i", t=PACK)
-            if g == 0:
-                nc.scalar.mul(ordered, raw, -1.0)
-                codes = held("w2_c0", [P, H], I32)
-                nc.vector.quantize_mx(codes[:].bitcast(FP8X4), w2_s[g][:], w2_rounded[g][:])
-                w2_c.append([codes[:, span(t, P)] for t in range(PACK)])
-                continue
             nc.vector.tensor_scalar(ordered[:, :, 0:2], raw[:, :, 0:2], -1.0, None, ALU.mult)
             nc.scalar.mul(ordered[:, :, 2:4], raw[:, :, 2:4], -1.0)
-            w2_c.append([])
-            for u, tag in enumerate(("w2_c1", "w3_raw")):
-                codes = held("w2_c1", [P, H // 2], I32, tag)
-                nc.vector.quantize_mx(
-                    codes[:].bitcast(FP8X4), w2_s[g][:, span(u, H // 2)], w2_rounded[g][:, span(u, PACK * H // 2)]
-                )
-                w2_c[g].extend(codes[:, span(t, P)] for t in range(2))
+
+        def quantize_w2(g, first, count, tag):
+            codes = held("w2_c", [P, count * P], I32, tag)
+            columns = slice(first * P, (first + count) * P)
+            words = slice(PACK * first * P, PACK * (first + count) * P)
+            nc.vector.quantize_mx(codes[:].bitcast(FP8X4), w2_s[g][:, columns], w2_rounded[g][:, words])
+            for t in range(count):
+                w2_c[g, first + t] = codes[:, span(t, P)]
+
+        round_w2(0)
+        quantize_w2(0, 0, PACK, "w2_c0")
+        w3_s = held("w3_s", [P, PASSES * H], U8)
+        reorder_columns(w3_s[:], w3_s_raw[:], 16)
+        round_w2(1)
+        quantize_w2(1, 0, 2, "w2_c1")
+        w3_c = held("w3_c", [P, PASSES * H], I32)
+        reorder_columns(w3_c[:], w3_raw[:], 4)
 
         page_rounded = [held("page_rounded%d" % c, [P, N, PACK], BF16) for c in range(CHUNKS)]
 
-        def product(banks, piece, passes):
+        def product(number, piece, passes):
             half = piece % HALVES
-            acc = bank(banks[piece % len(banks)])
-            for i, (codes, scales, g, v_scales) in enumerate(passes):
+            acc = bank(number)
+            for i, (codes, scales, g) in enumerate(passes):
                 nc.tensor.matmul_mx(
                     acc[:], lhsT=codes, lhsT_scale=scales, rhs=v_w[g][half][:].bitcast(FP8X4),
-                    rhs_scale=v_scales[g][:, span(half, N)], start=i == 0, stop=i == len(passes) - 1,
+                    rhs_scale=v_s[:, span(HALVES * g + half, N)], start=i == 0, stop=i == len(passes) - 1,
                 )
             return acc
 
-        def refill(t, half):
-            piece = HALVES * t + half
-            by_difference = piece in DIFFERENCE_PIECES
-            blocks = [PACK * g + t for g in range(PASSES)]
-            passes_a = [(w1_slice(t, g), w_s[:, span(blocks[g], P)], g, v_s_from_row0) for g in range(PASSES)]
-            passes_b = [(w2_c[g][t].bitcast(FP8X4), w2_s[g][:, span(t, P)], g, v_s) for g in range(PASSES)]
-            passes_c = [
-                (w3_c[:, span(blocks[g], P)].bitcast(FP8X4), w_s[4:, span(blocks[g], P)], g, v_s) for g in range(PASSES)
+        def passes_a(t):
+            return [
+                (w1_c[:].bitcast(U8)[:, span(PACK * g + t, 2 * P)].bitcast(FP4X4), w1_s[:, span(PACK * g + t, P)], g)
+                for g in range(PASSES)
             ]
-            acc_a = product(BANKS["a"], piece, passes_a)
-            if piece == 0:
-                a_sb = held("a_sb", [P, N], F32, "a_then_w1")
+
+        def passes_b(t):
+            return [(w2_c[g, t].bitcast(FP8X4), w2_s[g][:, span(t, P)], g) for g in range(PASSES)]
+
+        def passes_c(t):
+            return [
+                (w3_c[:, span(PACK * g + t, P)].bitcast(FP8X4), w3_s[:, span(PACK * g + t, P)], g) for g in range(PASSES)
+            ]
+
+        turns = {name: [] for name in FIRST_BANKS}
+
+        def next_bank(name):
+            turns[name].append(0)
+            return FIRST_BANKS[name][(len(turns[name]) - 1) % len(FIRST_BANKS[name])]
+
+        early_a = held("early_a", [P, EARLY_PIECES * N], F32, "w2_raw0")
+
+        def refill(piece):
+            t, half = divmod(piece, HALVES)
+            by_difference = piece in DIFFERENCE_PIECES
+            acc_a = product(next_bank("a then c" if piece < EARLY_PIECES else "c then a"), piece, passes_a(t))
+            if piece < EARLY_PIECES:
+                a_sb = early_a[:, span(piece, N)]
             else:
                 a_sb = ring.tile([P, N], F32, name="a_sb", tag="a_then_x")
             nc.scalar.copy(a_sb[:], acc_a[:])
-            if not by_difference:
-                acc_b = product(BANKS["b"], piece, passes_b)
-            else:
-                acc_b = product(BANKS["a"][::-1], piece, passes_a + passes_b)
+            if by_difference:
+                acc_b = product(next_bank("c then a"), piece, passes_a(t) + passes_b(t))
                 excess = ring.tile([P, N], F32, name="excess", bufs=len(DIFFERENCE_PIECES))
                 nc.scalar.activation(excess[:], acc_b[:], ACT.Relu)
-            acc_c = product(BANKS["c"], piece, passes_c)
-            weights = gain[piece][:]
-            fill = keep.tile([P, N], F32, name="fill", tag="c_then_fill%d" % (piece - 1 if piece > 1 else PIECES + piece))
+            else:
+                acc_b = product(next_bank("b"), piece, passes_b(t))
+            acc_c = product(next_bank("c then a" if piece < 2 else "a then c"), piece, passes_c(t))
+            least = held("least", [P, N], F32, "c%d" % (piece - 1 if piece > 1 else PIECES + piece))
+            target = page[t][:].indirect(list3[:, span(half, LIST_COLS)])
             if piece > 0:
-                c_sb = keep.tile([P, N], F32, name="c_sb", tag="c_then_fill%d" % piece)
+                c_sb = held("c_sb", [P, N], F32, "c%d" % piece)
                 nc.scalar.copy(c_sb[:], acc_c[:])
-                weighted = held("weighted", [P, N], F32, "gain%d" % (piece - 1))
-                nc.gpsimd.tensor_tensor(weighted[:], c_sb[:], weights, ALU.mult)
+                weighted = held("weighted", [P, N], F32, "gain%d" % (piece - 1) if piece > 1 else "weighted")
+                nc.gpsimd.tensor_tensor(weighted[:], c_sb[:], gain[piece][:], ALU.mult)
             if by_difference:
-                nc.gpsimd.tensor_tensor(fill[:], a_sb[:], excess[:], ALU.subtract)
+                nc.gpsimd.tensor_tensor(least[:], a_sb[:], excess[:], ALU.subtract)
             else:
-                nc.vector.scalar_tensor_tensor(fill[:], acc_b[:], -1.0, a_sb[:], ALU.mult, ALU.min)
+                nc.vector.scalar_tensor_tensor(least[:], acc_b[:], -1.0, a_sb[:], ALU.mult, ALU.min)
             if piece == 0:
-                nc.vector.tensor_tensor(fill[:], acc_c[:], fill[:], ALU.mult)
-                nc.vector.tensor_tensor(fill[:], fill[:], weights, ALU.mult)
-                order_w1(1, PACK - 1, "a_then_w1")
+                quantize_w2(1, 2, 2, "w3_raw")
+                parts = [span(u, N // 2) for u in range(2)]
+                for u in parts:
+                    nc.vector.tensor_tensor(least[:, u], acc_c[:, u], least[:, u], ALU.mult)
+                for u in parts:
+                    nc.vector.tensor_tensor(least[:, u], least[:, u], gain[piece][:, u], ALU.mult)
             else:
-                nc.gpsimd.tensor_tensor(fill[:], fill[:], weighted[:], ALU.mult)
-            nc.vector.tensor_copy(page[t][:].indirect(list3[:, span(half, LIST_COLS)]), fill[:])
+                nc.gpsimd.tensor_tensor(least[:], least[:], weighted[:], ALU.mult)
+            nc.vector.tensor_copy(target, least[:])
 
-        pairs = [held("pairs", [P, 2, N, 2], BF16, "w2_raw%d" % c) for c in range(VECTOR_CHUNKS)]
+        pairs = held("pairs", [P, 2, N, 2], BF16, "w2_raw1")
 
-        def round_slice(t):
-            for c in range(CHUNKS):
-                source = page[t][:, span(c, N)]
-                if c >= VECTOR_CHUNKS:
-                    nc.scalar.copy(page_rounded[c][:, :, t], source)
-                elif t < PACK - 2:
-                    nc.scalar.copy(pairs[c][:, 0, :, t], source)
-                elif t == PACK - 2:
-                    nc.scalar.copy(pairs[c][:, 1], source.unsqueeze(2).to_broadcast([P, N, 2]))
-                else:
-                    nc.vector.tensor_copy(pairs[c][:, 1, :, 1], source)
-            if t == PACK - 1:
-                for c in range(VECTOR_CHUNKS):
-                    nc.vector.tensor_copy(
-                        page_rounded[c][:].rearrange("p n t -> p (n t)").bitcast(I32).rearrange("p (n u) -> p n u", u=2),
-                        pairs[c][:].rearrange("p u n e -> p (u n e)").bitcast(I32).rearrange("p (u n) -> p n u", u=2),
-                    )
+        def round_chunk(t, c):
+            source = page[t][:, span(c, N)]
+            engine_copy = nc.vector.tensor_copy if t == PACK - 1 and c < VECTOR_CHUNKS else nc.scalar.copy
+            target = pairs[:, t // 2, :, :] if c == PAIR_CHUNK else page_rounded[c][:, :, span(t // 2, 2)]
+            if t == PACK - 2 and c < VECTOR_CHUNKS:
+                engine_copy(target, source.unsqueeze(2).to_broadcast([P, N, 2]))
+            else:
+                engine_copy(target[:, :, t % 2], source)
 
         v2_w = held("v2_w", [P, S2], I32)
-        v2_s = held("v2_s", [P, S2], U8)
-        for t in range(PACK):
-            for half in range(HALVES):
-                refill(t, half)
-            if t == PACK - 2:
+        for piece in range(PIECES):
+            t, half = divmod(piece, HALVES)
+            refill(piece)
+            if piece == PIECES - 2:
                 nc.vector.tensor_copy(v2_w[:].bitcast(U32), tab2_w[:].bitcast(U32).indirect(list2[:]))
-                nc.vector.tensor_copy(v2_s[:], tab2_s[:].indirect(list2[:]))
-            round_slice(t)
+            if half == HALVES - 1 and t < PACK - 1:
+                for c in range(CHUNKS):
+                    round_chunk(t, c)
 
         page_c = [held("page_c%d" % c, [P, N], I32) for c in range(CHUNKS)]
         page_s = [held("page_s%d" % c, [P, N], U8) for c in range(CHUNKS)]
-        for c in range(CHUNKS):
+
+        def quantize(c):
             words = page_rounded[c][:].rearrange("p n t -> p (n t)")
             nc.vector.quantize_mx(page_c[c][:].bitcast(FP8X4), page_s[c][:], words)
 
+        for c in (2, 3, 0, 1):
+            round_chunk(PACK - 1, c)
+        quantize(0)
+        nc.vector.tensor_copy(
+            page_rounded[PAIR_CHUNK][:].rearrange("p n t -> p (n t)").bitcast(I32).rearrange("p (n u) -> p n u", u=2),
+            pairs[:].rearrange("p u n e -> p (u n e)").bitcast(I32).rearrange("p (u n) -> p n u", u=2),
+        )
+        chunk_order = (0, 2, 1, 3)
+        for c in chunk_order[1:]:
+            quantize(c)
+
         e = [held("e%d" % n, [P, T2], F32) for n in range(GROUPS)]
+
+        def score(n, c, number):
+            acc_e = bank(number)
+            nc.tensor.matmul_mx(
+                acc_e[:], lhsT=v2_w[:, span(n, P)].bitcast(FP8X4), lhsT_scale=v2_s[:, span(n, P)],
+                rhs=page_c[c][:].bitcast(FP8X4), rhs_scale=page_s[c][:], start=True, stop=True,
+            )
+            if (n, c) in VECTOR_COPIES:
+                nc.vector.tensor_copy(e[n][:, span(c, N)], acc_e[:])
+            else:
+                nc.scalar.copy(e[n][:, span(c, N)], acc_e[:])
+
+        for i, c in enumerate(chunk_order):
+            for n in range(2):
+                score(n, c, EARLY_BANKS[n][i])
+        for i in range(2 * CHUNKS):
+            score(2 + i // CHUNKS, chunk_order[i % CHUNKS], LATE_BANKS[i % len(LATE_BANKS)])
         picked = []
         for n in range(GROUPS):
-            for c in range(CHUNKS):
-                acc_e = bank(c)
-                nc.tensor.matmul_mx(
-                    acc_e[:], lhsT=v2_w[:, span(n, P)].bitcast(FP8X4), lhsT_scale=v2_s[:, span(n, P)],
-                    rhs=page_c[c][:].bitcast(FP8X4), rhs_scale=page_s[c][:], start=True, stop=True,
-                )
-                if n == 0 and c >= CHUNKS - VECTOR_CHUNKS:
-                    nc.vector.tensor_copy(e[n][:, span(c, N)], acc_e[:])
-                else:
-                    nc.scalar.copy(e[n][:, span(c, N)], acc_e[:])
             for half in range(HALVES):
                 x = ring.tile([P, N], F32, name="x", tag="a_then_x")
                 nc.vector.tensor_copy(x[:], e[n][:].indirect(list4[:, span(half, LIST_COLS)]))
                 picked.append((n, half, x))
 
-        def square(x, piece, shares):
-            if piece < shares["gpsimd"]:
-                nc.gpsimd.tensor_tensor(x[:], x[:], x[:], ALU.mult)
-            elif piece < shares["gpsimd"] + shares["scalar"]:
+        def square(x, engine):
+            if engine is nc.scalar:
                 nc.scalar.activation(x[:], x[:], ACT.Square)
             else:
-                nc.vector.tensor_tensor(x[:], x[:], x[:], ALU.mult)
+                engine.tensor_tensor(x[:], x[:], x[:], ALU.mult)
 
-        for piece in range(FIRST_SQUARES["gpsimd"]):
-            square(picked[piece][2], piece, FIRST_SQUARES)
         for piece, (n, half, x) in enumerate(picked):
-            if piece >= FIRST_SQUARES["gpsimd"]:
-                square(x, piece, FIRST_SQUARES)
+            square(x, nc.gpsimd if piece in GPSIMD_FIRST_SQUARES else nc.vector)
             factor = inv_avail[:, n : n + 1]
             nc.scalar.activation(x[:], x[:], ACT.Abs_reciprocal_sqrt, bias=factor, scale=factor)
-            square(x, piece, SECOND_SQUARES)
+            square(x, nc.scalar if piece in SCALAR_SECOND_SQUARES else nc.vector)
             nc.sync.dma_start(out[span(n, P), span(half, N)], x[:])

@@ -34,11 +34,11 @@ VECTOR_CHUNKS = 2
 PAIR_CHUNK = 1
 GPSIMD_FIRST_SQUARES = range(6)
 SCALAR_SECOND_SQUARES = (0,1,2,3,7)
-VECTOR_COPIES = ((1, 0), (0, 3))
+VECTOR_COPIES = ((1, 0), (1, 2), (0, 3))
 BANKS = 8
 EARLY_PIECES = 3
-EARLY_BANKS = ((0, 1, 2, 3), (4, 5, 4, 6))
-LATE_BANKS = (3, 4, 6)
+EARLY_BANKS = ((0, 1, 2, 3), (4, 5, 4, 5))
+LATE_BANKS = (3, 4, 5)
 FIRST_BANKS = {"a then c": (0, 1, 2), "c then a": (3, 4), "b": (5, 6, 7)}
 
 
@@ -70,16 +70,14 @@ def tile_list_tow_dispatch_scores_kernel(
         tab2_s = held("tab2_s", [P, T3], U8)
         v_s = held("v_s", [P, PASSES * S], U8)
         v2_s = held("v2_s", [P, S2], U8)
-        w1_s_raw = held("w1_s_raw", [P, PASSES * H], U8)
-        w3_s_raw = held("w3_s_raw", [P, PASSES * H], U8)
+        w_s_raw = held("w_s_raw", [P, PASSES * H], U8)
         avail_rows = held("avail_rows", [P, P], F32)
         identity = held("identity", [P, P], F32)
-        nc.gpsimd.memset(tab_s[:].bitcast(I32), 0)
         nc.gpsimd.memset(avail_rows[:], 0.0)
+        nc.gpsimd.memset(tab_s[32:64, :].bitcast(I32), 0)
         make_identity(nc, identity[:])
-        nc.gpsimd.memset(tab2_s[:].bitcast(I32), 0)
-        for scales in (w1_s_raw, v_s, w3_s_raw, v2_s):
-            nc.vector.memset(scales[:].bitcast(I32), 0)
+        for scales in (w_s_raw[:], tab2_s[:], tab_s[64:128, :], v_s[:], v2_s[:]):
+            nc.vector.memset(scales.bitcast(I32), 0)
 
         tab_w = [held("tab_w%d" % g, [P, T], I32) for g in range(PASSES)]
         w1_raw = held("w1_raw", [P, PASSES * H // 2], I32)
@@ -95,11 +93,11 @@ def tile_list_tow_dispatch_scores_kernel(
         def load_w2(g):
             nc.sync.dma_start(w2_raw[g][:], w2[span(g, P * PACK), :].rearrange("(p i) r -> p i r", i=PACK))
 
-        def load_weight_scales(planes, scales):
-            rows = planes[:].bitcast(I32).rearrange("p (g r) -> p g r", g=PASSES)
+        def load_weight_scales(scales, first):
+            rows = w_s_raw[:].bitcast(I32).rearrange("p (g r) -> p g r", g=PASSES)
             for q in PORT_ORDER:
                 source = scales[:, span(q, 4), :].rearrange("g b r -> b g r")
-                nc.sync.dma_start(rows[32 * q : 32 * q + 4], source.bitcast(I32))
+                nc.sync.dma_start(rows[32 * q + first : 32 * q + first + 4], source.bitcast(I32))
 
         def load_gain(t, half):
             rows = wgs.rearrange("(m t) j -> m t j", t=PACK)
@@ -112,26 +110,26 @@ def tile_list_tow_dispatch_scores_kernel(
                 nc.sync.dma_start(target, rows[span(q, 4 * passes), :].bitcast(I32))
 
         nc.sync.dma_start(list1[:], offs)
-        nc.sync.dma_start(list3[:], offs3)
-        nc.scalar.dma_start(avail_rows[0:GROUPS, :], avail.rearrange("(n p) -> n p", p=P))
         nc.sync.dma_start(tab_s[0:32, :].bitcast(I32), tab_scales.rearrange("g q t -> q g t").bitcast(I32))
+        nc.sync.dma_start(avail_rows[0:GROUPS, :], avail.rearrange("(n p) -> n p", p=P))
         load_words(tab_w[0], tab_words[0])
         nc.gpsimd.dma_start(tab2_s[0:16, :].bitcast(I32), tab2_scales[0].bitcast(I32))
-        load_weight_scales(w1_s_raw, w1_scales)
-        load_words(tab_w[1], tab_words[1])
+        load_weight_scales(w1_scales, 0)
         nc.sync.dma_start(list2[:], offs2)
-        v_rows = held("v_rows", [P, S], U8)
-        nc.vector.tensor_copy(v_rows[:], tab_s[:].indirect(list1[:]))
-        spread_scale_rows(v_s, v_rows, PASSES)
         nc.sync.dma_start(
             w1_raw[:].rearrange("p (g r) -> p g r", g=PASSES), w1_words.rearrange("g p r -> p g r").bitcast(I32)
         )
         load_w2(0)
-        load_weight_scales(w3_s_raw, w3_scales)
+        load_weight_scales(w3_scales, 4)
+        load_words(tab_w[1], tab_words[1])
+        v_rows = held("v_rows", [P, S], U8)
+        nc.vector.tensor_copy(v_rows[:], tab_s[:].indirect(list1[:]))
+        spread_scale_rows(v_s, v_rows, PASSES)
         load_w2(1)
         nc.sync.dma_start(
             w3_raw[:].rearrange("p (g r) -> p g r", g=PASSES), w3_words.rearrange("g p r i -> p g (r i)").bitcast(I32)
         )
+        nc.sync.dma_start(list3[:], offs3)
         page_rows = page0.rearrange("(p t) c -> p t c", t=PACK)
         for t in range(PACK):
             load_gain(t, 0)
@@ -162,11 +160,11 @@ def tile_list_tow_dispatch_scores_kernel(
 
         w1_c = held("w1_c", [P, PASSES * H // 2], I32)
         reorder_columns(w1_c[:].bitcast(U16), w1_raw[:].bitcast(U16), 8)
-        v2_rows = held("v2_rows", [P, S2], U8, "w1_raw")
+        v2_rows = held("v2_rows", [P, S2], U8)
         nc.vector.tensor_copy(v2_rows[:], tab2_s[:].indirect(list2[:]))
         spread_scale_rows(v2_s, v2_rows, 1)
-        w1_s = held("w1_s", [P, PASSES * H], U8)
-        reorder_columns(w1_s[:], w1_s_raw[:], 16)
+        w_s = held("w_s", [P, PASSES * H], U8)
+        reorder_columns(w_s[:], w_s_raw[:], 16)
 
         w2_rounded = [held("w2_rounded%d" % g, [P, PACK * H], BF16) for g in range(PASSES)]
         w2_s = [held("w2_s%d" % g, [P, H], U8) for g in range(PASSES)]
@@ -175,6 +173,9 @@ def tile_list_tow_dispatch_scores_kernel(
         def round_w2(g):
             ordered = w2_rounded[g][:].rearrange("p (t m i) -> p m t i", t=PACK, i=PACK)
             raw = w2_raw[g][:].rearrange("p i (m t) -> p m t i", t=PACK)
+            if g == 0:
+                nc.scalar.mul(ordered, raw, -1.0)
+                return
             nc.vector.tensor_scalar(ordered[:, :, 0:2], raw[:, :, 0:2], -1.0, None, ALU.mult)
             nc.scalar.mul(ordered[:, :, 2:4], raw[:, :, 2:4], -1.0)
 
@@ -187,9 +188,7 @@ def tile_list_tow_dispatch_scores_kernel(
                 w2_c[g, first + t] = codes[:, span(t, P)]
 
         round_w2(0)
-        quantize_w2(0, 0, PACK, "w2_c0")
-        w3_s = held("w3_s", [P, PASSES * H], U8)
-        reorder_columns(w3_s[:], w3_s_raw[:], 16)
+        quantize_w2(0, 0, PACK, "w_s_raw")
         round_w2(1)
         quantize_w2(1, 0, 2, "w2_c1")
         w3_c = held("w3_c", [P, PASSES * H], I32)
@@ -197,19 +196,29 @@ def tile_list_tow_dispatch_scores_kernel(
 
         page_rounded = [held("page_rounded%d" % c, [P, N, PACK], BF16) for c in range(CHUNKS)]
 
-        def product(number, piece, passes):
+        def run_passes(acc, piece, passes, first, last):
             half = piece % HALVES
-            acc = bank(number)
-            for i, (codes, scales, g) in enumerate(passes):
+            for i in range(first, last):
+                codes, scales, g = passes[i]
                 nc.tensor.matmul_mx(
                     acc[:], lhsT=codes, lhsT_scale=scales, rhs=v_w[g][half][:].bitcast(FP8X4),
                     rhs_scale=v_s[:, span(HALVES * g + half, N)], start=i == 0, stop=i == len(passes) - 1,
                 )
+
+        opened = {}
+
+        def product(name, role, piece, passes):
+            if (name, piece) in opened:
+                acc = opened[name, piece]
+                run_passes(acc, piece, passes, 1, len(passes))
+            else:
+                acc = bank(next_bank(role))
+                run_passes(acc, piece, passes, 0, len(passes))
             return acc
 
         def passes_a(t):
             return [
-                (w1_c[:].bitcast(U8)[:, span(PACK * g + t, 2 * P)].bitcast(FP4X4), w1_s[:, span(PACK * g + t, P)], g)
+                (w1_c[:].bitcast(U8)[:, span(PACK * g + t, 2 * P)].bitcast(FP4X4), w_s[:, span(PACK * g + t, P)], g)
                 for g in range(PASSES)
             ]
 
@@ -218,7 +227,7 @@ def tile_list_tow_dispatch_scores_kernel(
 
         def passes_c(t):
             return [
-                (w3_c[:, span(PACK * g + t, P)].bitcast(FP8X4), w3_s[:, span(PACK * g + t, P)], g) for g in range(PASSES)
+                (w3_c[:, span(PACK * g + t, P)].bitcast(FP8X4), w_s[4:, span(PACK * g + t, P)], g) for g in range(PASSES)
             ]
 
         turns = {name: [] for name in FIRST_BANKS}
@@ -227,47 +236,60 @@ def tile_list_tow_dispatch_scores_kernel(
             turns[name].append(0)
             return FIRST_BANKS[name][(len(turns[name]) - 1) % len(FIRST_BANKS[name])]
 
-        early_a = held("early_a", [P, EARLY_PIECES * N], F32, "w2_raw0")
+        early_a = held("early_a", [P, HALVES * N], F32, "w2_raw0")
 
         def refill(piece):
             t, half = divmod(piece, HALVES)
             by_difference = piece in DIFFERENCE_PIECES
-            acc_a = product(next_bank("a then c" if piece < EARLY_PIECES else "c then a"), piece, passes_a(t))
-            if piece < EARLY_PIECES:
+            acc_a = product("a", "a then c" if piece < EARLY_PIECES else "c then a", piece, passes_a(t))
+            if piece < HALVES:
                 a_sb = early_a[:, span(piece, N)]
+            elif piece == HALVES:
+                a_sb = held("a_sb", [P, N], F32, "w2_raw1")
             else:
                 a_sb = ring.tile([P, N], F32, name="a_sb", tag="a_then_x")
             nc.scalar.copy(a_sb[:], acc_a[:])
             if by_difference:
-                acc_b = product(next_bank("c then a"), piece, passes_a(t) + passes_b(t))
+                acc_b = product("d", "c then a", piece, passes_a(t) + passes_b(t))
                 excess = ring.tile([P, N], F32, name="excess", bufs=len(DIFFERENCE_PIECES))
                 nc.scalar.activation(excess[:], acc_b[:], ACT.Relu)
             else:
-                acc_b = product(next_bank("b"), piece, passes_b(t))
-            acc_c = product(next_bank("c then a" if piece < 2 else "a then c"), piece, passes_c(t))
-            least = held("least", [P, N], F32, "c%d" % (piece - 1 if piece > 1 else PIECES + piece))
-            target = page[t][:].indirect(list3[:, span(half, LIST_COLS)])
+                acc_b = product("b", "b", piece, passes_b(t))
+            acc_c = product("c", "c then a" if piece < 2 else "a then c", piece, passes_c(t))
+            least = held("least", [P, N], F32, "gain0" if piece == 2 else "c%d" % ((piece - 1) % PIECES if piece != 1 else 1 + PIECES))
             if piece > 0:
                 c_sb = held("c_sb", [P, N], F32, "c%d" % piece)
                 nc.scalar.copy(c_sb[:], acc_c[:])
-                weighted = held("weighted", [P, N], F32, "gain%d" % (piece - 1) if piece > 1 else "weighted")
-                nc.gpsimd.tensor_tensor(weighted[:], c_sb[:], gain[piece][:], ALU.mult)
+                weighted = held("weighted", [P, N], F32, "gain%d" % (piece - 1))
+                if piece > 1:
+                    nc.gpsimd.tensor_tensor(weighted[:], c_sb[:], gain[piece][:], ALU.mult)
             if by_difference:
                 nc.gpsimd.tensor_tensor(least[:], a_sb[:], excess[:], ALU.subtract)
             else:
                 nc.vector.scalar_tensor_tensor(least[:], acc_b[:], -1.0, a_sb[:], ALU.mult, ALU.min)
             if piece == 0:
-                quantize_w2(1, 2, 2, "w3_raw")
                 parts = [span(u, N // 2) for u in range(2)]
                 for u in parts:
                     nc.vector.tensor_tensor(least[:, u], acc_c[:, u], least[:, u], ALU.mult)
                 for u in parts:
                     nc.vector.tensor_tensor(least[:, u], least[:, u], gain[piece][:, u], ALU.mult)
-            else:
+            elif piece == 1:
+                quantize_w2(1, 2, 2, "w3_raw")
+                nc.gpsimd.tensor_tensor(weighted[:], least[:], c_sb[:], ALU.mult)
+                nc.gpsimd.tensor_tensor(least[:], weighted[:], gain[piece][:], ALU.mult)
+            elif piece < PIECES - 1:
                 nc.gpsimd.tensor_tensor(least[:], least[:], weighted[:], ALU.mult)
-            nc.vector.tensor_copy(target, least[:])
+            return least, weighted if piece == PIECES - 1 else None
 
-        pairs = held("pairs", [P, 2, N, 2], BF16, "w2_raw1")
+        def scatter(piece, least, weighted):
+            t, half = divmod(piece, HALVES)
+            target = page[t][:].indirect(list3[:, span(half, LIST_COLS)])
+            if weighted is None:
+                nc.vector.tensor_copy(target, least[:])
+            else:
+                nc.vector.tensor_tensor(target, least[:], weighted[:], ALU.mult)
+
+        pairs = held("pairs", [P, 2, N, 2], BF16, "w2_raw0")
 
         def round_chunk(t, c):
             source = page[t][:, span(c, N)]
@@ -279,9 +301,16 @@ def tile_list_tow_dispatch_scores_kernel(
                 engine_copy(target[:, :, t % 2], source)
 
         v2_w = held("v2_w", [P, S2], I32)
+        for name, role, piece in [("a", "a then c", 0), ("a", "a then c", 1), ("b", "b", 0), ("b", "b", 1)]:
+            opened[name, piece] = bank(next_bank(role))
+            t = piece // HALVES
+            run_passes(opened[name, piece], piece, passes_a(t) if name == "a" else passes_b(t)[:1] + [None], 0, 1)
+        ready = [refill(0)]
         for piece in range(PIECES):
             t, half = divmod(piece, HALVES)
-            refill(piece)
+            if piece + 1 < PIECES:
+                ready.append(refill(piece + 1))
+            scatter(piece, *ready[piece])
             if piece == PIECES - 2:
                 nc.vector.tensor_copy(v2_w[:].bitcast(U32), tab2_w[:].bitcast(U32).indirect(list2[:]))
             if half == HALVES - 1 and t < PACK - 1:

@@ -33,12 +33,12 @@ DIFFERENCE_PIECES = (3, 5, 7)
 VECTOR_CHUNKS = 2
 PAIR_CHUNK = 1
 GPSIMD_FIRST_SQUARES = range(6)
-SCALAR_SECOND_SQUARES = (0,1,2,3,7)
-VECTOR_COPIES = ((1, 0), (1, 2), (0, 3))
+SCALAR_SECOND_SQUARES = (0, 1, 2, 3, 7)
+VECTOR_COPIES = ((1, 2), (0, 3))
 BANKS = 8
 EARLY_PIECES = 3
-EARLY_BANKS = ((0, 1, 2, 3), (4, 5, 4, 5))
-LATE_BANKS = (3, 4, 5)
+EARLY_BANKS = ((0, 1, 2, 3), (4, 5, 5, 7))
+LATE_BANKS = (3, 5, 7)
 FIRST_BANKS = {"a then c": (0, 1, 2), "c then a": (3, 4), "b": (5, 6, 7)}
 
 
@@ -269,12 +269,13 @@ def tile_list_tow_dispatch_scores_kernel(
                 nc.vector.scalar_tensor_tensor(least[:], acc_b[:], -1.0, a_sb[:], ALU.mult, ALU.min)
             if piece == 0:
                 parts = [span(u, N // 2) for u in range(2)]
-                for u in parts:
-                    nc.vector.tensor_tensor(least[:, u], acc_c[:, u], least[:, u], ALU.mult)
-                for u in parts:
-                    nc.vector.tensor_tensor(least[:, u], least[:, u], gain[piece][:, u], ALU.mult)
+                h = [held("h", [P, N // 2], F32, "h%d" % u) for u in range(2)]
+                for u, part in enumerate(parts):
+                    nc.vector.tensor_tensor(h[u][:], acc_c[:, part], least[:, part], ALU.mult)
+                for u, part in enumerate(parts):
+                    nc.vector.tensor_tensor(least[:, part], h[u][:], gain[piece][:, part], ALU.mult)
+                quantize_w2(1, 2, 2, "h0")
             elif piece == 1:
-                quantize_w2(1, 2, 2, "w3_raw")
                 nc.gpsimd.tensor_tensor(weighted[:], least[:], c_sb[:], ALU.mult)
                 nc.gpsimd.tensor_tensor(least[:], weighted[:], gain[piece][:], ALU.mult)
             elif piece < PIECES - 1:
@@ -300,7 +301,14 @@ def tile_list_tow_dispatch_scores_kernel(
             else:
                 engine_copy(target[:, :, t % 2], source)
 
-        v2_w = held("v2_w", [P, S2], I32)
+        v2_w = []
+
+        def gather_trucks(tag):
+            words = held("v2_w", [P, S2 // 2], I32, tag)
+            entries = list2[:, span(len(v2_w), LIST_COLS // 2)]
+            nc.vector.tensor_copy(words[:].bitcast(U32), tab2_w[:].bitcast(U32).indirect(entries))
+            v2_w.append(words)
+
         for name, role, piece in [("a", "a then c", 0), ("a", "a then c", 1), ("b", "b", 0), ("b", "b", 1)]:
             opened[name, piece] = bank(next_bank(role))
             t = piece // HALVES
@@ -311,8 +319,8 @@ def tile_list_tow_dispatch_scores_kernel(
             if piece + 1 < PIECES:
                 ready.append(refill(piece + 1))
             scatter(piece, *ready[piece])
-            if piece == PIECES - 2:
-                nc.vector.tensor_copy(v2_w[:].bitcast(U32), tab2_w[:].bitcast(U32).indirect(list2[:]))
+            if piece >= PIECES - 2:
+                gather_trucks("gain%d" % piece if piece == PIECES - 1 else "v2_w")
             if half == HALVES - 1 and t < PACK - 1:
                 for c in range(CHUNKS):
                     round_chunk(t, c)
@@ -340,7 +348,7 @@ def tile_list_tow_dispatch_scores_kernel(
         def score(n, c, number):
             acc_e = bank(number)
             nc.tensor.matmul_mx(
-                acc_e[:], lhsT=v2_w[:, span(n, P)].bitcast(FP8X4), lhsT_scale=v2_s[:, span(n, P)],
+                acc_e[:], lhsT=v2_w[n // 2][:, span(n % 2, P)].bitcast(FP8X4), lhsT_scale=v2_s[:, span(n, P)],
                 rhs=page_c[c][:].bitcast(FP8X4), rhs_scale=page_s[c][:], start=True, stop=True,
             )
             if (n, c) in VECTOR_COPIES:

@@ -36,7 +36,7 @@ GPSIMD_FIRST_SQUARES = range(6)
 SCALAR_SECOND_SQUARES = (0, 1, 2, 3, 7)
 VECTOR_COPIES = ((1, 2), (0, 3))
 BANKS = 8
-EARLY_PIECES = 3
+EARLY_PIECES = 2
 EARLY_BANKS = ((0, 1, 2, 3), (4, 5, 5, 7))
 LATE_BANKS = (3, 5, 7)
 FIRST_BANKS = {"a then c": (0, 1, 2), "c then a": (3, 4), "b": (5, 6, 7)}
@@ -74,9 +74,9 @@ def tile_list_tow_dispatch_scores_kernel(
         avail_rows = held("avail_rows", [P, P], F32)
         identity = held("identity", [P, P], F32)
         nc.gpsimd.memset(avail_rows[:], 0.0)
-        nc.gpsimd.memset(tab_s[32:64, :].bitcast(I32), 0)
         make_identity(nc, identity[:])
-        for scales in (w_s_raw[:], tab2_s[:], tab_s[64:128, :], v_s[:], v2_s[:]):
+        nc.gpsimd.memset(w_s_raw[:].bitcast(I32), 0)
+        for scales in (tab_s[32:64, :], tab_s[64:128, :], tab2_s[:], v_s[:], v2_s[:]):
             nc.vector.memset(scales.bitcast(I32), 0)
 
         tab_w = [held("tab_w%d" % g, [P, T], I32) for g in range(PASSES)]
@@ -97,7 +97,7 @@ def tile_list_tow_dispatch_scores_kernel(
             rows = w_s_raw[:].bitcast(I32).rearrange("p (g r) -> p g r", g=PASSES)
             for q in PORT_ORDER:
                 source = scales[:, span(q, 4), :].rearrange("g b r -> b g r")
-                nc.sync.dma_start(rows[32 * q + first : 32 * q + first + 4], source.bitcast(I32))
+                nc.gpsimd.dma_start(rows[32 * q + first : 32 * q + first + 4], source.bitcast(I32))
 
         def load_gain(t, half):
             rows = wgs.rearrange("(m t) j -> m t j", t=PACK)
@@ -113,14 +113,14 @@ def tile_list_tow_dispatch_scores_kernel(
         nc.sync.dma_start(tab_s[0:32, :].bitcast(I32), tab_scales.rearrange("g q t -> q g t").bitcast(I32))
         nc.sync.dma_start(avail_rows[0:GROUPS, :], avail.rearrange("(n p) -> n p", p=P))
         load_words(tab_w[0], tab_words[0])
-        nc.gpsimd.dma_start(tab2_s[0:16, :].bitcast(I32), tab2_scales[0].bitcast(I32))
         load_weight_scales(w1_scales, 0)
-        nc.sync.dma_start(list2[:], offs2)
+        load_weight_scales(w3_scales, 4)
         nc.sync.dma_start(
             w1_raw[:].rearrange("p (g r) -> p g r", g=PASSES), w1_words.rearrange("g p r -> p g r").bitcast(I32)
         )
         load_w2(0)
-        load_weight_scales(w3_scales, 4)
+        nc.sync.dma_start(tab2_s[16:32, :].bitcast(I32), tab2_scales[0].bitcast(I32))
+        nc.sync.dma_start(list2[:], offs2)
         load_words(tab_w[1], tab_words[1])
         v_rows = held("v_rows", [P, S], U8)
         nc.vector.tensor_copy(v_rows[:], tab_s[:].indirect(list1[:]))
@@ -162,8 +162,8 @@ def tile_list_tow_dispatch_scores_kernel(
         reorder_columns(w1_c[:].bitcast(U16), w1_raw[:].bitcast(U16), 8)
         v2_rows = held("v2_rows", [P, S2], U8)
         nc.vector.tensor_copy(v2_rows[:], tab2_s[:].indirect(list2[:]))
-        spread_scale_rows(v2_s, v2_rows, 1)
-        w_s = held("w_s", [P, PASSES * H], U8)
+        spread_scale_rows(v2_s, v2_rows[16:32, :], 1)
+        w_s = held("w_s", [P, PASSES * H], U8, "tab_w1")
         reorder_columns(w_s[:], w_s_raw[:], 16)
 
         w2_rounded = [held("w2_rounded%d" % g, [P, PACK * H], BF16) for g in range(PASSES)]
@@ -188,7 +188,7 @@ def tile_list_tow_dispatch_scores_kernel(
                 w2_c[g, first + t] = codes[:, span(t, P)]
 
         round_w2(0)
-        quantize_w2(0, 0, PACK, "w_s_raw")
+        quantize_w2(0, 0, PACK, "w2_c0")
         round_w2(1)
         quantize_w2(1, 0, 2, "w2_c1")
         w3_c = held("w3_c", [P, PASSES * H], I32)
@@ -309,7 +309,7 @@ def tile_list_tow_dispatch_scores_kernel(
             nc.vector.tensor_copy(words[:].bitcast(U32), tab2_w[:].bitcast(U32).indirect(entries))
             v2_w.append(words)
 
-        for name, role, piece in [("a", "a then c", 0), ("a", "a then c", 1), ("b", "b", 0), ("b", "b", 1)]:
+        for name, role, piece in [("b", "b", 0), ("b", "b", 1), ("b", "b", 2)]:
             opened[name, piece] = bank(next_bank(role))
             t = piece // HALVES
             run_passes(opened[name, piece], piece, passes_a(t) if name == "a" else passes_b(t)[:1] + [None], 0, 1)

@@ -70,13 +70,14 @@ def tile_list_tow_dispatch_scores_kernel(
         tab2_s = held("tab2_s", [P, T3], U8)
         v_s = held("v_s", [P, PASSES * S], U8)
         v2_s = held("v2_s", [P, S2], U8)
-        w_s_raw = held("w_s_raw", [P, PASSES * H], U8)
+        w1_s_raw = held("w1_s_raw", [P, PASSES * H], U8)
+        w3_s_raw = held("w3_s_raw", [P, PASSES * H], U8)
         avail_rows = held("avail_rows", [P, P], F32)
         identity = held("identity", [P, P], F32)
         nc.gpsimd.memset(avail_rows[:], 0.0)
         make_identity(nc, identity[:])
-        nc.gpsimd.memset(w_s_raw[:].bitcast(I32), 0)
-        for scales in (tab_s[32:64, :], tab_s[64:128, :], tab2_s[:], v_s[:], v2_s[:]):
+        nc.gpsimd.memset(w1_s_raw[:].bitcast(I32), 0)
+        for scales in (tab_s[32:64, :], tab_s[64:128, :], tab2_s[:], v_s[:], v2_s[:], w3_s_raw[:]):
             nc.vector.memset(scales.bitcast(I32), 0)
 
         tab_w = [held("tab_w%d" % g, [P, T], I32) for g in range(PASSES)]
@@ -93,11 +94,11 @@ def tile_list_tow_dispatch_scores_kernel(
         def load_w2(g):
             nc.sync.dma_start(w2_raw[g][:], w2[span(g, P * PACK), :].rearrange("(p i) r -> p i r", i=PACK))
 
-        def load_weight_scales(scales, first):
-            rows = w_s_raw[:].bitcast(I32).rearrange("p (g r) -> p g r", g=PASSES)
-            for q in PORT_ORDER:
-                source = scales[:, span(q, 4), :].rearrange("g b r -> b g r")
-                nc.gpsimd.dma_start(rows[32 * q + first : 32 * q + first + 4], source.bitcast(I32))
+        def load_weight_scales(scales, planes, first):
+            rows = planes[:].bitcast(I32).rearrange("p (g r) -> p g r", g=PASSES)
+            for b in range(4):
+                source = scales[:, b:16:4, :].rearrange("g q r -> q g r")
+                nc.gpsimd.dma_start(rows[first + b : P : 32], source.bitcast(I32))
 
         def load_gain(t, half):
             rows = wgs.rearrange("(m t) j -> m t j", t=PACK)
@@ -107,24 +108,24 @@ def tile_list_tow_dispatch_scores_kernel(
         def spread_scale_rows(planes, rows, passes):
             for q in PORT_ORDER:
                 target = planes[32 * q : 32 * q + 4, :].bitcast(I32).rearrange("p (g j) -> p g j", g=passes)
-                nc.sync.dma_start(target, rows[span(q, 4 * passes), :].bitcast(I32))
+                nc.sync.dma_start(target, rows(q).bitcast(I32))
 
         nc.sync.dma_start(list1[:], offs)
         nc.sync.dma_start(tab_s[0:32, :].bitcast(I32), tab_scales.rearrange("g q t -> q g t").bitcast(I32))
         nc.sync.dma_start(avail_rows[0:GROUPS, :], avail.rearrange("(n p) -> n p", p=P))
         load_words(tab_w[0], tab_words[0])
-        load_weight_scales(w1_scales, 0)
-        load_weight_scales(w3_scales, 4)
+        load_weight_scales(w1_scales, w1_s_raw, 0)
+        load_weight_scales(w3_scales, w3_s_raw, 4)
         nc.sync.dma_start(
             w1_raw[:].rearrange("p (g r) -> p g r", g=PASSES), w1_words.rearrange("g p r -> p g r").bitcast(I32)
         )
         load_w2(0)
-        nc.sync.dma_start(tab2_s[16:32, :].bitcast(I32), tab2_scales[0].bitcast(I32))
+        nc.sync.dma_start(tab2_s[4:P:8, :].bitcast(I32), tab2_scales[0].bitcast(I32))
         nc.sync.dma_start(list2[:], offs2)
         load_words(tab_w[1], tab_words[1])
         v_rows = held("v_rows", [P, S], U8)
         nc.vector.tensor_copy(v_rows[:], tab_s[:].indirect(list1[:]))
-        spread_scale_rows(v_s, v_rows, PASSES)
+        spread_scale_rows(v_s, lambda q: v_rows[span(q, 4 * PASSES), :], PASSES)
         load_w2(1)
         nc.sync.dma_start(
             w3_raw[:].rearrange("p (g r) -> p g r", g=PASSES), w3_words.rearrange("g p r i -> p g (r i)").bitcast(I32)
@@ -162,9 +163,11 @@ def tile_list_tow_dispatch_scores_kernel(
         reorder_columns(w1_c[:].bitcast(U16), w1_raw[:].bitcast(U16), 8)
         v2_rows = held("v2_rows", [P, S2], U8)
         nc.vector.tensor_copy(v2_rows[:], tab2_s[:].indirect(list2[:]))
-        spread_scale_rows(v2_s, v2_rows[16:32, :], 1)
-        w_s = held("w_s", [P, PASSES * H], U8, "tab_w1")
-        reorder_columns(w_s[:], w_s_raw[:], 16)
+        spread_scale_rows(v2_s, lambda q: v2_rows[32 * q + 4 : 32 * (q + 1) : 8, :], 1)
+        w1_s = held("w1_s", [P, PASSES * H], U8, "tab2_s")
+        reorder_columns(w1_s[:], w1_s_raw[:], 16)
+        w3_s = held("w3_s", [P, PASSES * H], U8, "tab_w1")
+        reorder_columns(w3_s[:], w3_s_raw[:], 16)
 
         w2_rounded = [held("w2_rounded%d" % g, [P, PACK * H], BF16) for g in range(PASSES)]
         w2_s = [held("w2_s%d" % g, [P, H], U8) for g in range(PASSES)]
@@ -218,7 +221,7 @@ def tile_list_tow_dispatch_scores_kernel(
 
         def passes_a(t):
             return [
-                (w1_c[:].bitcast(U8)[:, span(PACK * g + t, 2 * P)].bitcast(FP4X4), w_s[:, span(PACK * g + t, P)], g)
+                (w1_c[:].bitcast(U8)[:, span(PACK * g + t, 2 * P)].bitcast(FP4X4), w1_s[:, span(PACK * g + t, P)], g)
                 for g in range(PASSES)
             ]
 
@@ -227,7 +230,7 @@ def tile_list_tow_dispatch_scores_kernel(
 
         def passes_c(t):
             return [
-                (w3_c[:, span(PACK * g + t, P)].bitcast(FP8X4), w_s[4:, span(PACK * g + t, P)], g) for g in range(PASSES)
+                (w3_c[:, span(PACK * g + t, P)].bitcast(FP8X4), w3_s[4:, span(PACK * g + t, P)], g) for g in range(PASSES)
             ]
 
         turns = {name: [] for name in FIRST_BANKS}
@@ -309,7 +312,7 @@ def tile_list_tow_dispatch_scores_kernel(
             nc.vector.tensor_copy(words[:].bitcast(U32), tab2_w[:].bitcast(U32).indirect(entries))
             v2_w.append(words)
 
-        for name, role, piece in [("b", "b", 0), ("b", "b", 1), ("b", "b", 2)]:
+        for name, role, piece in [("a", "a then c", 0), ("a", "a then c", 1), ("b", "b", 0), ("b", "b", 1)]:
             opened[name, piece] = bank(next_bank(role))
             t = piece // HALVES
             run_passes(opened[name, piece], piece, passes_a(t) if name == "a" else passes_b(t)[:1] + [None], 0, 1)

@@ -32,9 +32,11 @@ PIECES = PACK * HALVES
 DIFFERENCE_PIECES = (3, 5, 7)
 VECTOR_CHUNKS = 2
 PAIR_CHUNK = 1
-GPSIMD_FIRST_SQUARES = range(6)
-SCALAR_SECOND_SQUARES = (0, 1, 2, 3, 7)
+FIRST_SQUARES = "GGGGGGVV"
+SECOND_SQUARES = "SSSSVVVS"
 VECTOR_COPIES = ((1, 2), (0, 3))
+CUTS = ((0, N), (N, N))
+LAST_CUTS = CUTS
 BANKS = 8
 EARLY_PIECES = 2
 EARLY_BANKS = ((0, 1, 2, 3), (4, 5, 5, 7))
@@ -74,17 +76,18 @@ def tile_list_tow_dispatch_scores_kernel(
         w3_s_raw = held("w3_s_raw", [P, PASSES * H], U8)
         avail_rows = held("avail_rows", [P, P], F32)
         identity = held("identity", [P, P], F32)
+        gain_rows = held("gain_rows", [P, N], F32)
         nc.gpsimd.memset(avail_rows[:], 0.0)
         make_identity(nc, identity[:])
         nc.gpsimd.memset(w1_s_raw[:].bitcast(I32), 0)
-        for scales in (tab_s[32:64, :], tab_s[64:128, :], tab2_s[:], v_s[:], v2_s[:], w3_s_raw[:]):
+        for scales in (tab_s[32:64, :], tab_s[64:128, :], gain_rows[:], tab2_s[:], v_s[:], v2_s[:], w3_s_raw[:]):
             nc.vector.memset(scales.bitcast(I32), 0)
 
         tab_w = [held("tab_w%d" % g, [P, T], I32) for g in range(PASSES)]
         w1_raw = held("w1_raw", [P, PASSES * H // 2], I32)
         w2_raw = [held("w2_raw%d" % g, [P, PACK, H], F32) for g in range(PASSES)]
         w3_raw = held("w3_raw", [P, PASSES * H], I32)
-        gain = [held("gain%d" % piece, [P, N], F32) for piece in range(PIECES)]
+        gain = {}
         page = [held("page%d" % t, [P, T2], F32) for t in range(PACK)]
         tab2_w = held("tab2_w", [P, T3], I32)
 
@@ -100,20 +103,31 @@ def tile_list_tow_dispatch_scores_kernel(
                 source = scales[:, b:16:4, :].rearrange("g q r -> q g r")
                 nc.gpsimd.dma_start(rows[first + b : P : 32], source.bitcast(I32))
 
+        def load_scale_rows(rows, scales):
+            nc.sync.dma_start(rows.bitcast(I32), scales.rearrange("g q t -> q g t").bitcast(I32))
+
+        def reorder_columns(ordered, raw, run, copy):
+            copy(
+                ordered.rearrange("p (g t m j) -> p g m t j", g=PASSES, t=PACK, j=run),
+                raw.rearrange("p (g m j t) -> p g m t j", g=PASSES, t=PACK, j=run),
+            )
+
         def load_gain(t, half):
             rows = wgs.rearrange("(m t) j -> m t j", t=PACK)
+            gain[HALVES * t + half] = held("gain", [P, N], F32, "gain%d" % (HALVES * t + half))
             for q in PORT_ORDER:
                 nc.sync.dma_start(gain[HALVES * t + half][span(q, 32), :], rows[:, t, span(half, N)])
 
-        def spread_scale_rows(planes, rows, passes):
+        def spread_scale_rows(queue, planes, rows, passes):
             for q in PORT_ORDER:
                 target = planes[32 * q : 32 * q + 4, :].bitcast(I32).rearrange("p (g j) -> p g j", g=passes)
-                nc.sync.dma_start(target, rows(q).bitcast(I32))
+                queue.dma_start(target, rows(q).bitcast(I32))
 
         nc.sync.dma_start(list1[:], offs)
-        nc.sync.dma_start(tab_s[0:32, :].bitcast(I32), tab_scales.rearrange("g q t -> q g t").bitcast(I32))
+        load_scale_rows(tab_s[0:32, :], tab_scales)
         nc.sync.dma_start(avail_rows[0:GROUPS, :], avail.rearrange("(n p) -> n p", p=P))
         load_words(tab_w[0], tab_words[0])
+        nc.sync.dma_start(gain_rows[0:32, :], wgs.rearrange("(m t) j -> m t j", t=PACK)[:, 0, 0:N])
         load_weight_scales(w1_scales, w1_s_raw, 0)
         load_weight_scales(w3_scales, w3_s_raw, 4)
         nc.sync.dma_start(
@@ -125,7 +139,7 @@ def tile_list_tow_dispatch_scores_kernel(
         load_words(tab_w[1], tab_words[1])
         v_rows = held("v_rows", [P, S], U8)
         nc.vector.tensor_copy(v_rows[:], tab_s[:].indirect(list1[:]))
-        spread_scale_rows(v_s, lambda q: v_rows[span(q, 4 * PASSES), :], PASSES)
+        spread_scale_rows(nc.sync, v_s, lambda q: v_rows[span(q, 4 * PASSES), :], PASSES)
         load_w2(1)
         nc.sync.dma_start(
             w3_raw[:].rearrange("p (g r) -> p g r", g=PASSES), w3_words.rearrange("g p r i -> p g (r i)").bitcast(I32)
@@ -133,7 +147,8 @@ def tile_list_tow_dispatch_scores_kernel(
         nc.sync.dma_start(list3[:], offs3)
         page_rows = page0.rearrange("(p t) c -> p t c", t=PACK)
         for t in range(PACK):
-            load_gain(t, 0)
+            if t > 0:
+                load_gain(t, 0)
             nc.sync.dma_start(page[t][:], page_rows[:, t, :])
             if t == PACK - 1:
                 load_words(tab2_w, tab2_words[0])
@@ -147,57 +162,69 @@ def tile_list_tow_dispatch_scores_kernel(
         nc.scalar.activation(root[:], avail_cols[:, 0:GROUPS], ACT.Abs_reciprocal_sqrt)
         nc.scalar.activation(inv_avail[:], root[:], ACT.Square)
 
+        turned = bank(3)
+        for u in range(N // P):
+            nc.tensor.transpose(turned[:, span(u, P)], gain_rows[:, span(u, P)], identity[:])
+        repeated = held("repeated", [P, N], F32, "gain0")
+        nc.scalar.copy(
+            repeated[:].rearrange("p (u q m) -> p u q m", q=QUADRANTS, m=32),
+            turned[:].rearrange("p (u r) -> p u r", r=P)[:, :, 0:32].unsqueeze(2).to_broadcast([P, N // P, QUADRANTS, 32]),
+        )
+        gain[0] = bank(2)
+        for u in range(N // P):
+            nc.tensor.transpose(gain[0][:, span(u, P)], repeated[:, span(u, P)], identity[:])
+
         v_w = [[held("v_w%d_%d" % (g, half), [P, N], I32) for half in range(HALVES)] for g in range(PASSES)]
         for g in range(PASSES):
             for half in range(HALVES):
                 window = tab_w[g][:].bitcast(U32)
                 nc.vector.tensor_copy(v_w[g][half][:].bitcast(U32), window.indirect(list1[:, span(half, LIST_COLS)]))
 
-        def reorder_columns(ordered, raw, run):
-            nc.vector.tensor_copy(
-                ordered.rearrange("p (g t m j) -> p g m t j", g=PASSES, t=PACK, j=run),
-                raw.rearrange("p (g m j t) -> p g m t j", g=PASSES, t=PACK, j=run),
-            )
-
         w1_c = held("w1_c", [P, PASSES * H // 2], I32)
-        reorder_columns(w1_c[:].bitcast(U16), w1_raw[:].bitcast(U16), 8)
+        reorder_columns(w1_c[:].bitcast(U16), w1_raw[:].bitcast(U16), 8, nc.vector.tensor_copy)
         v2_rows = held("v2_rows", [P, S2], U8)
         nc.vector.tensor_copy(v2_rows[:], tab2_s[:].indirect(list2[:]))
-        spread_scale_rows(v2_s, lambda q: v2_rows[32 * q + 4 : 32 * (q + 1) : 8, :], 1)
-        w1_s = held("w1_s", [P, PASSES * H], U8, "tab2_s")
-        reorder_columns(w1_s[:], w1_s_raw[:], 16)
-        w3_s = held("w3_s", [P, PASSES * H], U8, "tab_w1")
-        reorder_columns(w3_s[:], w3_s_raw[:], 16)
+        spread_scale_rows(nc.sync, v2_s, lambda q: v2_rows[32 * q + 4 : 32 * (q + 1) : 8, :], 1)
 
-        w2_rounded = [held("w2_rounded%d" % g, [P, PACK * H], BF16) for g in range(PASSES)]
+        w1_s = held("w1_s", [P, PASSES * H], U8, "tab_w1")
+        reorder_columns(w1_s[:], w1_s_raw[:], 16, nc.vector.tensor_copy)
+
         w2_s = [held("w2_s%d" % g, [P, H], U8) for g in range(PASSES)]
         w2_c = {}
 
-        def round_w2(g):
-            ordered = w2_rounded[g][:].rearrange("p (t m i) -> p m t i", t=PACK, i=PACK)
-            raw = w2_raw[g][:].rearrange("p i (m t) -> p m t i", t=PACK)
-            if g == 0:
+        def round_w2(g, first, count, engine):
+            rounded = held("w2_rounded%d_%d" % (g, first), [P, count * PACK * P], BF16)
+            ordered = rounded[:].rearrange("p (t m i) -> p m t i", t=count, i=PACK)
+            raw = w2_raw[g][:].rearrange("p i (m t) -> p m t i", t=PACK)[:, :, first : first + count]
+            if engine is nc.scalar:
                 nc.scalar.mul(ordered, raw, -1.0)
-                return
-            nc.vector.tensor_scalar(ordered[:, :, 0:2], raw[:, :, 0:2], -1.0, None, ALU.mult)
-            nc.scalar.mul(ordered[:, :, 2:4], raw[:, :, 2:4], -1.0)
+            else:
+                nc.vector.tensor_scalar(ordered, raw, -1.0, None, ALU.mult)
+            return rounded
 
-        def quantize_w2(g, first, count, tag):
-            codes = held("w2_c", [P, count * P], I32, tag)
-            columns = slice(first * P, (first + count) * P)
-            words = slice(PACK * first * P, PACK * (first + count) * P)
-            nc.vector.quantize_mx(codes[:].bitcast(FP8X4), w2_s[g][:, columns], w2_rounded[g][:, words])
+        def quantize_w2(g, first, count, rounded, tag=None):
+            codes = held("w2_c%d_%d" % (g, first), [P, count * P], I32, tag)
+            nc.vector.quantize_mx(codes[:].bitcast(FP8X4), w2_s[g][:, first * P : (first + count) * P], rounded[:])
             for t in range(count):
                 w2_c[g, first + t] = codes[:, span(t, P)]
 
-        round_w2(0)
-        quantize_w2(0, 0, PACK, "w2_c0")
-        round_w2(1)
-        quantize_w2(1, 0, 2, "w2_c1")
-        w3_c = held("w3_c", [P, PASSES * H], I32)
-        reorder_columns(w3_c[:], w3_raw[:], 4)
+        quantize_w2(0, 0, PACK, round_w2(0, 0, PACK, nc.scalar))
+        front = round_w2(1, 0, 2, nc.vector)
+        back = round_w2(1, 2, 2, nc.scalar)
+        quantize_w2(1, 0, 2, front)
+        w3_c = [held("w3_c%d" % u, [P, PASSES * H // 2], I32, (None, "w3_s_raw")[u]) for u in range(2)]
+        w3_by_slice = w3_raw[:].bitcast(U32).rearrange("p (g m j t) -> p g m t j", g=PASSES, t=PACK, j=4)
 
-        page_rounded = [held("page_rounded%d" % c, [P, N, PACK], BF16) for c in range(CHUNKS)]
+        def reorder_w3(u, copy):
+            ordered = w3_c[u][:].bitcast(U32).rearrange("p (g t m j) -> p g m t j", g=PASSES, t=2, j=4)
+            copy(ordered, w3_by_slice[:, :, :, span(u, 2)])
+
+        w3_s = held("w3_s", [P, PASSES * H], U8, "w2_rounded1_0")
+        reorder_columns(w3_s[:], w3_s_raw[:], 16, nc.vector.tensor_copy)
+        reorder_w3(0, nc.vector.tensor_copy)
+
+        spent = ("v_w0_1", None, "w3_s_raw", "w1_c")
+        page_rounded = [held("page_rounded%d" % c, [P, N, PACK], BF16, spent[c]) for c in range(CHUNKS)]
 
         def run_passes(acc, piece, passes, first, last):
             half = piece % HALVES
@@ -230,7 +257,7 @@ def tile_list_tow_dispatch_scores_kernel(
 
         def passes_c(t):
             return [
-                (w3_c[:, span(PACK * g + t, P)].bitcast(FP8X4), w3_s[4:, span(PACK * g + t, P)], g) for g in range(PASSES)
+                (w3_c[t // 2][:, span(2 * g + t % 2, P)].bitcast(FP8X4), w3_s[4:, span(PACK * g + t, P)], g) for g in range(PASSES)
             ]
 
         turns = {name: [] for name in FIRST_BANKS}
@@ -239,7 +266,7 @@ def tile_list_tow_dispatch_scores_kernel(
             turns[name].append(0)
             return FIRST_BANKS[name][(len(turns[name]) - 1) % len(FIRST_BANKS[name])]
 
-        early_a = held("early_a", [P, HALVES * N], F32, "w2_raw0")
+        early_a = held("early_a", [P, HALVES * N], F32, "w2_raw1")
 
         def refill(piece):
             t, half = divmod(piece, HALVES)
@@ -247,8 +274,6 @@ def tile_list_tow_dispatch_scores_kernel(
             acc_a = product("a", "a then c" if piece < EARLY_PIECES else "c then a", piece, passes_a(t))
             if piece < HALVES:
                 a_sb = early_a[:, span(piece, N)]
-            elif piece == HALVES:
-                a_sb = held("a_sb", [P, N], F32, "w2_raw1")
             else:
                 a_sb = ring.tile([P, N], F32, name="a_sb", tag="a_then_x")
             nc.scalar.copy(a_sb[:], acc_a[:])
@@ -259,11 +284,11 @@ def tile_list_tow_dispatch_scores_kernel(
             else:
                 acc_b = product("b", "b", piece, passes_b(t))
             acc_c = product("c", "c then a" if piece < 2 else "a then c", piece, passes_c(t))
-            least = held("least", [P, N], F32, "gain0" if piece == 2 else "c%d" % ((piece - 1) % PIECES if piece != 1 else 1 + PIECES))
+            least = held("least", [P, N], F32, {1: "gain0", 2: "h1"}.get(piece, "c%d" % ((piece - 1) % PIECES)))
             if piece > 0:
                 c_sb = held("c_sb", [P, N], F32, "c%d" % piece)
                 nc.scalar.copy(c_sb[:], acc_c[:])
-                weighted = held("weighted", [P, N], F32, "gain%d" % (piece - 1))
+                weighted = held("weighted", [P, N], F32, "gain%d" % (piece - 1) if piece > 1 else "h1")
                 if piece > 1:
                     nc.gpsimd.tensor_tensor(weighted[:], c_sb[:], gain[piece][:], ALU.mult)
             if by_difference:
@@ -277,7 +302,7 @@ def tile_list_tow_dispatch_scores_kernel(
                     nc.vector.tensor_tensor(h[u][:], acc_c[:, part], least[:, part], ALU.mult)
                 for u, part in enumerate(parts):
                     nc.vector.tensor_tensor(least[:, part], h[u][:], gain[piece][:, part], ALU.mult)
-                quantize_w2(1, 2, 2, "h0")
+                quantize_w2(1, 2, 2, back, "h0")
             elif piece == 1:
                 nc.gpsimd.tensor_tensor(weighted[:], least[:], c_sb[:], ALU.mult)
                 nc.gpsimd.tensor_tensor(least[:], weighted[:], gain[piece][:], ALU.mult)
@@ -293,7 +318,7 @@ def tile_list_tow_dispatch_scores_kernel(
             else:
                 nc.vector.tensor_tensor(target, least[:], weighted[:], ALU.mult)
 
-        pairs = held("pairs", [P, 2, N, 2], BF16, "w2_raw0")
+        pairs = held("pairs", [P, 2, N, 2], BF16, "v_w1_1")
 
         def round_chunk(t, c):
             source = page[t][:, span(c, N)]
@@ -312,7 +337,7 @@ def tile_list_tow_dispatch_scores_kernel(
             nc.vector.tensor_copy(words[:].bitcast(U32), tab2_w[:].bitcast(U32).indirect(entries))
             v2_w.append(words)
 
-        for name, role, piece in [("a", "a then c", 0), ("a", "a then c", 1), ("b", "b", 0), ("b", "b", 1)]:
+        for name, role, piece in [("b", "b", 0), ("b", "b", 1), ("a", "a then c", 0), ("a", "a then c", 1)]:
             opened[name, piece] = bank(next_bank(role))
             t = piece // HALVES
             run_passes(opened[name, piece], piece, passes_a(t) if name == "a" else passes_b(t)[:1] + [None], 0, 1)
@@ -321,12 +346,14 @@ def tile_list_tow_dispatch_scores_kernel(
             t, half = divmod(piece, HALVES)
             if piece + 1 < PIECES:
                 ready.append(refill(piece + 1))
+            if piece == 0:
+                reorder_w3(1, nc.scalar.copy)
             scatter(piece, *ready[piece])
             if piece >= PIECES - 2:
                 gather_trucks("gain%d" % piece if piece == PIECES - 1 else "v2_w")
-            if half == HALVES - 1 and t < PACK - 1:
-                for c in range(CHUNKS):
-                    round_chunk(t, c)
+        for t in range(PACK - 1):
+            for c in range(CHUNKS):
+                round_chunk(t, c)
 
         page_c = [held("page_c%d" % c, [P, N], I32) for c in range(CHUNKS)]
         page_s = [held("page_s%d" % c, [P, N], U8) for c in range(CHUNKS)]
@@ -366,10 +393,10 @@ def tile_list_tow_dispatch_scores_kernel(
             score(2 + i // CHUNKS, chunk_order[i % CHUNKS], LATE_BANKS[i % len(LATE_BANKS)])
         picked = []
         for n in range(GROUPS):
-            for half in range(HALVES):
-                x = ring.tile([P, N], F32, name="x", tag="a_then_x")
-                nc.vector.tensor_copy(x[:], e[n][:].indirect(list4[:, span(half, LIST_COLS)]))
-                picked.append((n, half, x))
+            for first, count in (LAST_CUTS if n == GROUPS - 1 else CUTS):
+                x = ring.tile([P, count], F32, name="x", tag="a_then_x")
+                nc.vector.tensor_copy(x[:], e[n][:].indirect(list4[:, first // 16 : (first + count) // 16]))
+                picked.append((n, slice(first, first + count), x))
 
         def square(x, engine):
             if engine is nc.scalar:
@@ -377,9 +404,10 @@ def tile_list_tow_dispatch_scores_kernel(
             else:
                 engine.tensor_tensor(x[:], x[:], x[:], ALU.mult)
 
-        for piece, (n, half, x) in enumerate(picked):
-            square(x, nc.gpsimd if piece in GPSIMD_FIRST_SQUARES else nc.vector)
+        engines = {"S": nc.scalar, "V": nc.vector, "G": nc.gpsimd}
+        for piece, (n, columns, x) in enumerate(picked):
+            square(x, engines[FIRST_SQUARES[piece]])
             factor = inv_avail[:, n : n + 1]
             nc.scalar.activation(x[:], x[:], ACT.Abs_reciprocal_sqrt, bias=factor, scale=factor)
-            square(x, nc.scalar if piece in SCALAR_SECOND_SQUARES else nc.vector)
-            nc.sync.dma_start(out[span(n, P), span(half, N)], x[:])
+            square(x, engines[SECOND_SQUARES[piece]])
+            nc.sync.dma_start(out[span(n, P), columns], x[:])

@@ -279,7 +279,7 @@ def tile_list_tow_dispatch_scores_kernel(
             nc.scalar.copy(a_sb[:], acc_a[:])
             if by_difference:
                 acc_b = product("d", "c then a", piece, passes_a(t) + passes_b(t))
-                excess = ring.tile([P, N], F32, name="excess", bufs=len(DIFFERENCE_PIECES))
+                excess = held("excess%d" % piece, [P, N], F32)
                 nc.scalar.activation(excess[:], acc_b[:], ACT.Relu)
             else:
                 acc_b = product("b", "b", piece, passes_b(t))
@@ -318,11 +318,14 @@ def tile_list_tow_dispatch_scores_kernel(
             else:
                 nc.vector.tensor_tensor(target, least[:], weighted[:], ALU.mult)
 
-        pairs = held("pairs", [P, 2, N, 2], BF16, "v_w1_1")
+        def gpsimd_round(target, source):
+            nc.gpsimd.tensor_scalar(target, source, 1.0, 0.0, ALU.mult, ALU.add)
 
         def round_chunk(t, c):
             source = page[t][:, span(c, N)]
             engine_copy = nc.vector.tensor_copy if t == PACK - 1 and c < VECTOR_CHUNKS else nc.scalar.copy
+            if t < 2 and c == PAIR_CHUNK:
+                engine_copy = gpsimd_round
             target = pairs[:, t // 2, :, :] if c == PAIR_CHUNK else page_rounded[c][:, :, span(t // 2, 2)]
             if t == PACK - 2 and c < VECTOR_CHUNKS:
                 engine_copy(target, source.unsqueeze(2).to_broadcast([P, N, 2]))
@@ -351,6 +354,7 @@ def tile_list_tow_dispatch_scores_kernel(
             scatter(piece, *ready[piece])
             if piece >= PIECES - 2:
                 gather_trucks("gain%d" % piece if piece == PIECES - 1 else "v2_w")
+        pairs = held("pairs", [P, 2, N, 2], BF16, "excess%d" % (PIECES - 1))
         for t in range(PACK - 1):
             for c in range(CHUNKS):
                 round_chunk(t, c)

@@ -80,7 +80,7 @@ def tile_list_tow_dispatch_scores_kernel(
         nc.gpsimd.memset(avail_rows[:], 0.0)
         make_identity(nc, identity[:])
         nc.gpsimd.memset(w1_s_raw[:].bitcast(I32), 0)
-        for scales in (tab_s[32:64, :], tab_s[64:128, :], gain_rows[:], tab2_s[:], v_s[:], v2_s[:], w3_s_raw[:]):
+        for scales in (tab2_s[:], tab_s[32:64, :], tab_s[64:128, :], gain_rows[:], v_s[:], v2_s[:], w3_s_raw[:]):
             nc.vector.memset(scales.bitcast(I32), 0)
 
         tab_w = [held("tab_w%d" % g, [P, T], I32) for g in range(PASSES)]
@@ -127,15 +127,15 @@ def tile_list_tow_dispatch_scores_kernel(
         load_scale_rows(tab_s[0:32, :], tab_scales)
         nc.sync.dma_start(avail_rows[0:GROUPS, :], avail.rearrange("(n p) -> n p", p=P))
         load_words(tab_w[0], tab_words[0])
+        nc.sync.dma_start(tab2_s[4:P:8, :].bitcast(I32), tab2_scales[0].bitcast(I32))
+        nc.sync.dma_start(list2[:], offs2)
+        load_w2(0)
         nc.sync.dma_start(gain_rows[0:32, :], wgs.rearrange("(m t) j -> m t j", t=PACK)[:, 0, 0:N])
         load_weight_scales(w1_scales, w1_s_raw, 0)
         load_weight_scales(w3_scales, w3_s_raw, 4)
         nc.sync.dma_start(
             w1_raw[:].rearrange("p (g r) -> p g r", g=PASSES), w1_words.rearrange("g p r -> p g r").bitcast(I32)
         )
-        load_w2(0)
-        nc.sync.dma_start(tab2_s[4:P:8, :].bitcast(I32), tab2_scales[0].bitcast(I32))
-        nc.sync.dma_start(list2[:], offs2)
         load_words(tab_w[1], tab_words[1])
         v_rows = held("v_rows", [P, S], U8)
         nc.vector.tensor_copy(v_rows[:], tab_s[:].indirect(list1[:]))
@@ -170,7 +170,7 @@ def tile_list_tow_dispatch_scores_kernel(
             repeated[:].rearrange("p (u q m) -> p u q m", q=QUADRANTS, m=32),
             turned[:].rearrange("p (u r) -> p u r", r=P)[:, :, 0:32].unsqueeze(2).to_broadcast([P, N // P, QUADRANTS, 32]),
         )
-        gain[0] = bank(2)
+        gain[0] = bank(7)
         for u in range(N // P):
             nc.tensor.transpose(gain[0][:, span(u, P)], repeated[:, span(u, P)], identity[:])
 

@@ -52,6 +52,7 @@ def tile_list_tow_dispatch_scores_kernel(
     with ExitStack() as ctx:
         keep = ctx.enter_context(tc.tile_pool(name="keep", bufs=1))
         ring = ctx.enter_context(tc.tile_pool(name="ring", bufs=PIECES))
+        laid = ctx.enter_context(tc.tile_pool(name="laid", bufs=1))
         psum = ctx.enter_context(tc.psum_pool(name="psum", bufs=1))
 
         def bank(number):
@@ -88,7 +89,8 @@ def tile_list_tow_dispatch_scores_kernel(
         w2_raw = [held("w2_raw%d" % g, [P, PACK, H], F32) for g in range(PASSES)]
         w3_raw = held("w3_raw", [P, PASSES * H], I32)
         gain = {}
-        page = [held("page%d" % t, [P, T2], F32) for t in range(PACK)]
+        page = [held("page%d" % t, [P, T2], F32) for t in range(PACK) if t != PACK - 2]
+        page.insert(PACK - 2, laid.tile([P, T2], F32, name="page2", offset=0, align_bytes=64))
         tab2_w = held("tab2_w", [P, T3], I32)
 
         def load_words(tile, words):
@@ -114,7 +116,10 @@ def tile_list_tow_dispatch_scores_kernel(
 
         def load_gain(t, half):
             rows = wgs.rearrange("(m t) j -> m t j", t=PACK)
-            gain[HALVES * t + half] = held("gain", [P, N], F32, "gain%d" % (HALVES * t + half))
+            if HALVES * t + half == PIECES - 1:
+                gain[PIECES - 1] = laid.tile([P, N], F32, name="last_gain", offset=4 * T2, align_bytes=64)
+            else:
+                gain[HALVES * t + half] = held("gain", [P, N], F32, "gain%d" % (HALVES * t + half))
             for q in PORT_ORDER:
                 nc.sync.dma_start(gain[HALVES * t + half][span(q, 32), :], rows[:, t, span(half, N)])
 
@@ -327,15 +332,11 @@ def tile_list_tow_dispatch_scores_kernel(
             if t < 2 and c == PAIR_CHUNK:
                 engine_copy = gpsimd_round
             target = pairs[:, t // 2, :, :] if c == PAIR_CHUNK else page_rounded[c][:, :, span(t // 2, 2)]
-            if t == PACK - 2 and c < VECTOR_CHUNKS:
-                engine_copy(target, source.unsqueeze(2).to_broadcast([P, N, 2]))
-            else:
-                engine_copy(target[:, :, t % 2], source)
+            engine_copy(target[:, :, t % 2], source)
 
         v2_w = []
 
-        def gather_trucks(tag):
-            words = held("v2_w", [P, S2 // 2], I32, tag)
+        def gather_trucks(words):
             entries = list2[:, span(len(v2_w), LIST_COLS // 2)]
             nc.vector.tensor_copy(words[:].bitcast(U32), tab2_w[:].bitcast(U32).indirect(entries))
             v2_w.append(words)
@@ -352,12 +353,13 @@ def tile_list_tow_dispatch_scores_kernel(
             if piece == 0:
                 reorder_w3(1, nc.scalar.copy)
             scatter(piece, *ready[piece])
-            if piece >= PIECES - 2:
-                gather_trucks("gain%d" % piece if piece == PIECES - 1 else "v2_w")
+            if piece == PIECES - 2:
+                gather_trucks(held("v2_w", [P, S2 // 2], I32))
         pairs = held("pairs", [P, 2, N, 2], BF16, "excess%d" % (PIECES - 1))
         for t in range(PACK - 1):
             for c in range(CHUNKS):
                 round_chunk(t, c)
+        gather_trucks(laid.tile([P, S2 // 2], I32, name="v2_w_last", offset=4 * T2 - S2, align_bytes=64))
 
         page_c = [held("page_c%d" % c, [P, N], I32) for c in range(CHUNKS)]
         page_s = [held("page_s%d" % c, [P, N], U8) for c in range(CHUNKS)]

from contextlib import ExitStack

import concourse.mybir as mybir
from concourse.masks import make_identity

K, T, S, H, T2, T3, S2, PICKED = 1024, 2048, 1024, 512, 2048, 2048, 512, 1024
FLOPS = 2 * (3 * K * H * S + H * S2 * T2)

F32 = mybir.dt.float32
BF16 = mybir.dt.bfloat16
I32 = mybir.dt.int32
U32 = mybir.dt.uint32
U16 = mybir.dt.uint16
U8 = mybir.dt.uint8
FP8X4 = mybir.dt.float8_e4m3fn_x4
FP4X4 = mybir.dt.float4_e2m1fn_x4
ALU = mybir.AluOpType
ACT = mybir.ActivationFunctionType

P = 128
N = 512
PACK = 4
PASSES = K // (P * PACK)
HALVES = S // N
CHUNKS = T2 // N
GROUPS = S2 // P
QUADRANTS = 4
PORT_ORDER = (0, 2, 1, 3)
LIST_COLS = N // 16

PIECES = PACK * HALVES
DIFFERENCE_PIECES = (3, 5, 7)
VECTOR_CHUNKS = 2
PAIR_CHUNK = 1
FIRST_SQUARES = "GGGGGGVV"
SECOND_SQUARES = "SSSSVVVS"
VECTOR_COPIES = ((1, 2), (0, 3))
CUTS = ((0, N), (N, N))
LAST_CUTS = CUTS
BANKS = 8
EARLY_PIECES = 2
EARLY_BANKS = ((0, 1, 2, 3), (4, 5, 5, 7))
LATE_BANKS = (3, 5, 7)
FIRST_BANKS = {"a then c": (0, 1, 2), "c then a": (3, 4), "b": (5, 6, 7)}


def tile_list_tow_dispatch_scores_kernel(
    tc, tab_words, tab_scales, tab2_words, tab2_scales, w1_words, w1_scales, w2,
    w3_words, w3_scales, page0, wgs, avail, offs, offs2, offs3, offs4, out,
):
    nc = tc.nc
    with ExitStack() as ctx:
        keep = ctx.enter_context(tc.tile_pool(name="keep", bufs=1))
        ring = ctx.enter_context(tc.tile_pool(name="ring", bufs=PIECES))
        laid = ctx.enter_context(tc.tile_pool(name="laid", bufs=1))
        psum = ctx.enter_context(tc.psum_pool(name="psum", bufs=1))

        def bank(number):
            return psum.tile([P, N], F32, name="acc", tag="bank%d" % number)

        def held(name, shape, dtype, tag=None):
            return keep.tile(shape, dtype, name=name, tag=tag or name, align_bytes=64)

        def span(i, width):
            return slice(width * i, width * (i + 1))

        list1 = held("list1", [P, S // 16], U16)
        list2 = held("list2", [P, S2 // 16], U16)
        list3 = held("list3", [P, S // 16], U16)
        list4 = held("list4", [P, PICKED // 16], U16)

        tab_s = held("tab_s", [P, T], U8)
        tab2_s = held("tab2_s", [P, T3], U8)
        v_s = held("v_s", [P, PASSES * S], U8)
        v2_s = held("v2_s", [P, S2], U8)
        w1_s_raw = held("w1_s_raw", [P, PASSES * H], U8)
        w3_s_raw = held("w3_s_raw", [P, PASSES * H], U8)
        avail_rows = held("avail_rows", [P, P], F32)
        identity = held("identity", [P, P], F32)
        gain_rows = held("gain_rows", [P, N], F32)
        nc.gpsimd.memset(avail_rows[:], 0.0)
        make_identity(nc, identity[:])
        nc.gpsimd.memset(w1_s_raw[:].bitcast(I32), 0)
        for scales in (tab2_s[:], tab_s[32:64, :], tab_s[64:128, :], gain_rows[:], v_s[:], v2_s[:], w3_s_raw[:]):
            nc.vector.memset(scales.bitcast(I32), 0)

        tab_w = [held("tab_w%d" % g, [P, T], I32) for g in range(PASSES)]
        w1_raw = held("w1_raw", [P, PASSES * H // 2], I32)
        w2_raw = [held("w2_raw%d" % g, [P, PACK, H], F32) for g in range(PASSES)]
        w3_raw = held("w3_raw", [P, PASSES * H], I32)
        gain = {}
        page = [held("page%d" % t, [P, T2], F32) for t in range(PACK) if t != PACK - 2]
        page.insert(PACK - 2, laid.tile([P, T2], F32, name="page2", offset=0, align_bytes=64))
        tab2_w = held("tab2_w", [P, T3], I32)

        def load_words(tile, words):
            nc.sync.dma_start(tile[:], words.rearrange("p t i -> p (t i)").bitcast(I32))

        def load_w2(g):
            nc.sync.dma_start(w2_raw[g][:], w2[span(g, P * PACK), :].rearrange("(p i) r -> p i r", i=PACK))

        def load_weight_scales(scales, planes, first):
            rows = planes[:].bitcast(I32).rearrange("p (g r) -> p g r", g=PASSES)
            for b in range(4):
                source = scales[:, b:16:4, :].rearrange("g q r -> q g r")
                nc.gpsimd.dma_start(rows[first + b : P : 32], source.bitcast(I32))

        def load_scale_rows(rows, scales):
            nc.sync.dma_start(rows.bitcast(I32), scales.rearrange("g q t -> q g t").bitcast(I32))

        def reorder_columns(ordered, raw, run, copy):
            copy(
                ordered.rearrange("p (g t m j) -> p g m t j", g=PASSES, t=PACK, j=run),
                raw.rearrange("p (g m j t) -> p g m t j", g=PASSES, t=PACK, j=run),
            )

        def load_gain(t, half):
            rows = wgs.rearrange("(m t) j -> m t j", t=PACK)
            if HALVES * t + half == PIECES - 1:
                gain[PIECES - 1] = laid.tile([P, N], F32, name="last_gain", offset=4 * T2, align_bytes=64)
            else:
                gain[HALVES * t + half] = held("gain", [P, N], F32, "gain%d" % (HALVES * t + half))
            for q in PORT_ORDER:
                nc.sync.dma_start(gain[HALVES * t + half][span(q, 32), :], rows[:, t, span(half, N)])

        def spread_scale_rows(queue, planes, rows, passes):
            for q in PORT_ORDER:
                target = planes[32 * q : 32 * q + 4, :].bitcast(I32).rearrange("p (g j) -> p g j", g=passes)
                queue.dma_start(target, rows(q).bitcast(I32))

        nc.sync.dma_start(list1[:], offs)
        load_scale_rows(tab_s[0:32, :], tab_scales)
        nc.sync.dma_start(avail_rows[0:GROUPS, :], avail.rearrange("(n p) -> n p", p=P))
        load_words(tab_w[0], tab_words[0])
        nc.sync.dma_start(tab2_s[4:P:8, :].bitcast(I32), tab2_scales[0].bitcast(I32))
        nc.sync.dma_start(list2[:], offs2)
        load_w2(0)
        nc.sync.dma_start(gain_rows[0:32, :], wgs.rearrange("(m t) j -> m t j", t=PACK)[:, 0, 0:N])
        load_weight_scales(w1_scales, w1_s_raw, 0)
        load_weight_scales(w3_scales, w3_s_raw, 4)
        nc.sync.dma_start(
            w1_raw[:].rearrange("p (g r) -> p g r", g=PASSES), w1_words.rearrange("g p r -> p g r").bitcast(I32)
        )
        load_words(tab_w[1], tab_words[1])
        v_rows = held("v_rows", [P, S], U8)
        nc.vector.tensor_copy(v_rows[:], tab_s[:].indirect(list1[:]))
        spread_scale_rows(nc.sync, v_s, lambda q: v_rows[span(q, 4 * PASSES), :], PASSES)
        load_w2(1)
        nc.sync.dma_start(
            w3_raw[:].rearrange("p (g r) -> p g r", g=PASSES), w3_words.rearrange("g p r i -> p g (r i)").bitcast(I32)
        )
        nc.sync.dma_start(list3[:], offs3)
        page_rows = page0.rearrange("(p t) c -> p t c", t=PACK)
        for t in range(PACK):
            if t > 0:
                load_gain(t, 0)
            nc.sync.dma_start(page[t][:], page_rows[:, t, :])
            if t == PACK - 1:
                load_words(tab2_w, tab2_words[0])
            load_gain(t, 1)
        nc.sync.dma_start(list4[:], offs4)

        root = held("root", [P, GROUPS], F32)
        inv_avail = held("inv_avail", [P, GROUPS], F32)
        avail_cols = bank(BANKS - 1)
        nc.tensor.transpose(avail_cols[:, 0:P], avail_rows[:], identity[:])
        nc.scalar.activation(root[:], avail_cols[:, 0:GROUPS], ACT.Abs_reciprocal_sqrt)
        nc.scalar.activation(inv_avail[:], root[:], ACT.Square)

        turned = bank(3)
        for u in range(N // P):
            nc.tensor.transpose(turned[:, span(u, P)], gain_rows[:, span(u, P)], identity[:])
        repeated = held("repeated", [P, N], F32, "gain0")
        nc.scalar.copy(
            repeated[:].rearrange("p (u q m) -> p u q m", q=QUADRANTS, m=32),
            turned[:].rearrange("p (u r) -> p u r", r=P)[:, :, 0:32].unsqueeze(2).to_broadcast([P, N // P, QUADRANTS, 32]),
        )
        gain[0] = bank(7)
        for u in range(N // P):
            nc.tensor.transpose(gain[0][:, span(u, P)], repeated[:, span(u, P)], identity[:])

        v_w = [[held("v_w%d_%d" % (g, half), [P, N], I32) for half in range(HALVES)] for g in range(PASSES)]
        for g in range(PASSES):
            for half in range(HALVES):
                window = tab_w[g][:].bitcast(U32)
                nc.vector.tensor_copy(v_w[g][half][:].bitcast(U32), window.indirect(list1[:, span(half, LIST_COLS)]))

        w1_c = held("w1_c", [P, PASSES * H // 2], I32)
        reorder_columns(w1_c[:].bitcast(U16), w1_raw[:].bitcast(U16), 8, nc.vector.tensor_copy)
        v2_rows = held("v2_rows", [P, S2], U8)
        nc.vector.tensor_copy(v2_rows[:], tab2_s[:].indirect(list2[:]))
        spread_scale_rows(nc.sync, v2_s, lambda q: v2_rows[32 * q + 4 : 32 * (q + 1) : 8, :], 1)

        w1_s = held("w1_s", [P, PASSES * H], U8, "tab_w1")
        reorder_columns(w1_s[:], w1_s_raw[:], 16, nc.vector.tensor_copy)

        w2_s = [held("w2_s%d" % g, [P, H], U8) for g in range(PASSES)]
        w2_c = {}

        def round_w2(g, first, count, engine):
            rounded = held("w2_rounded%d_%d" % (g, first), [P, count * PACK * P], BF16)
            ordered = rounded[:].rearrange("p (t m i) -> p m t i", t=count, i=PACK)
            raw = w2_raw[g][:].rearrange("p i (m t) -> p m t i", t=PACK)[:, :, first : first + count]
            if engine is nc.scalar:
                nc.scalar.mul(ordered, raw, -1.0)
            else:
                nc.vector.tensor_scalar(ordered, raw, -1.0, None, ALU.mult)
            return rounded

        def quantize_w2(g, first, count, rounded, tag=None):
            codes = held("w2_c%d_%d" % (g, first), [P, count * P], I32, tag)
            nc.vector.quantize_mx(codes[:].bitcast(FP8X4), w2_s[g][:, first * P : (first + count) * P], rounded[:])
            for t in range(count):
                w2_c[g, first + t] = codes[:, span(t, P)]

        quantize_w2(0, 0, PACK, round_w2(0, 0, PACK, nc.scalar))
        front = round_w2(1, 0, 2, nc.vector)
        back = round_w2(1, 2, 2, nc.scalar)
        quantize_w2(1, 0, 2, front)
        w3_c = [held("w3_c%d" % u, [P, PASSES * H // 2], I32, (None, "w3_s_raw")[u]) for u in range(2)]
        w3_by_slice = w3_raw[:].bitcast(U32).rearrange("p (g m j t) -> p g m t j", g=PASSES, t=PACK, j=4)

        def reorder_w3(u, copy):
            ordered = w3_c[u][:].bitcast(U32).rearrange("p (g t m j) -> p g m t j", g=PASSES, t=2, j=4)
            copy(ordered, w3_by_slice[:, :, :, span(u, 2)])

        w3_s = held("w3_s", [P, PASSES * H], U8, "w2_rounded1_0")
        reorder_columns(w3_s[:], w3_s_raw[:], 16, nc.vector.tensor_copy)
        reorder_w3(0, nc.vector.tensor_copy)

        spent = ("v_w0_1", None, "w3_s_raw", "w1_c")
        page_rounded = [held("page_rounded%d" % c, [P, N, PACK], BF16, spent[c]) for c in range(CHUNKS)]

        def run_passes(acc, piece, passes, first, last):
            half = piece % HALVES
            for i in range(first, last):
                codes, scales, g = passes[i]
                nc.tensor.matmul_mx(
                    acc[:], lhsT=codes, lhsT_scale=scales, rhs=v_w[g][half][:].bitcast(FP8X4),
                    rhs_scale=v_s[:, span(HALVES * g + half, N)], start=i == 0, stop=i == len(passes) - 1,
                )

        opened = {}

        def product(name, role, piece, passes):
            if (name, piece) in opened:
                acc = opened[name, piece]
                run_passes(acc, piece, passes, 1, len(passes))
            else:
                acc = bank(next_bank(role))
                run_passes(acc, piece, passes, 0, len(passes))
            return acc

        def passes_a(t):
            return [
                (w1_c[:].bitcast(U8)[:, span(PACK * g + t, 2 * P)].bitcast(FP4X4), w1_s[:, span(PACK * g + t, P)], g)
                for g in range(PASSES)
            ]

        def passes_b(t):
            return [(w2_c[g, t].bitcast(FP8X4), w2_s[g][:, span(t, P)], g) for g in range(PASSES)]

        def passes_c(t):
            return [
                (w3_c[t // 2][:, span(2 * g + t % 2, P)].bitcast(FP8X4), w3_s[4:, span(PACK * g + t, P)], g) for g in range(PASSES)
            ]

        turns = {name: [] for name in FIRST_BANKS}

        def next_bank(name):
            turns[name].append(0)
            return FIRST_BANKS[name][(len(turns[name]) - 1) % len(FIRST_BANKS[name])]

        early_a = held("early_a", [P, HALVES * N], F32, "w2_raw1")

        def refill(piece):
            t, half = divmod(piece, HALVES)
            by_difference = piece in DIFFERENCE_PIECES
            acc_a = product("a", "a then c" if piece < EARLY_PIECES else "c then a", piece, passes_a(t))
            if piece < HALVES:
                a_sb = early_a[:, span(piece, N)]
            else:
                a_sb = ring.tile([P, N], F32, name="a_sb", tag="a_then_x")
            nc.scalar.copy(a_sb[:], acc_a[:])
            if by_difference:
                acc_b = product("d", "c then a", piece, passes_a(t) + passes_b(t))
                excess = held("excess%d" % piece, [P, N], F32)
                nc.scalar.activation(excess[:], acc_b[:], ACT.Relu)
            else:
                acc_b = product("b", "b", piece, passes_b(t))
            acc_c = product("c", "c then a" if piece < 2 else "a then c", piece, passes_c(t))
            least = held("least", [P, N], F32, {1: "gain0", 2: "h1"}.get(piece, "c%d" % ((piece - 1) % PIECES)))
            if piece > 0:
                c_sb = held("c_sb", [P, N], F32, "c%d" % piece)
                nc.scalar.copy(c_sb[:], acc_c[:])
                weighted = held("weighted", [P, N], F32, "gain%d" % (piece - 1) if piece > 1 else "h1")
                if piece > 1:
                    nc.gpsimd.tensor_tensor(weighted[:], c_sb[:], gain[piece][:], ALU.mult)
            if by_difference:
                nc.gpsimd.tensor_tensor(least[:], a_sb[:], excess[:], ALU.subtract)
            else:
                nc.vector.scalar_tensor_tensor(least[:], acc_b[:], -1.0, a_sb[:], ALU.mult, ALU.min)
            if piece == 0:
                parts = [span(u, N // 2) for u in range(2)]
                h = [held("h", [P, N // 2], F32, "h%d" % u) for u in range(2)]
                for u, part in enumerate(parts):
                    nc.vector.tensor_tensor(h[u][:], acc_c[:, part], least[:, part], ALU.mult)
                for u, part in enumerate(parts):
                    nc.vector.tensor_tensor(least[:, part], h[u][:], gain[piece][:, part], ALU.mult)
                quantize_w2(1, 2, 2, back, "h0")
            elif piece == 1:
                nc.gpsimd.tensor_tensor(weighted[:], least[:], c_sb[:], ALU.mult)
                nc.gpsimd.tensor_tensor(least[:], weighted[:], gain[piece][:], ALU.mult)
            elif piece < PIECES - 1:
                nc.gpsimd.tensor_tensor(least[:], least[:], weighted[:], ALU.mult)
            return least, weighted if piece == PIECES - 1 else None

        def scatter(piece, least, weighted):
            t, half = divmod(piece, HALVES)
            target = page[t][:].indirect(list3[:, span(half, LIST_COLS)])
            if weighted is None:
                nc.vector.tensor_copy(target, least[:])
            else:
                nc.vector.tensor_tensor(target, least[:], weighted[:], ALU.mult)

        def gpsimd_round(target, source):
            nc.gpsimd.tensor_scalar(target, source, 1.0, 0.0, ALU.mult, ALU.add)

        def round_chunk(t, c):
            source = page[t][:, span(c, N)]
            engine_copy = nc.vector.tensor_copy if t == PACK - 1 and c < VECTOR_CHUNKS else nc.scalar.copy
            if t < 2 and c == PAIR_CHUNK:
                engine_copy = gpsimd_round
            target = pairs[:, t // 2, :, :] if c == PAIR_CHUNK else page_rounded[c][:, :, span(t // 2, 2)]
            engine_copy(target[:, :, t % 2], source)

        v2_w = []

        def gather_trucks(words):
            entries = list2[:, span(len(v2_w), LIST_COLS // 2)]
            nc.vector.tensor_copy(words[:].bitcast(U32), tab2_w[:].bitcast(U32).indirect(entries))
            v2_w.append(words)

        for name, role, piece in [("b", "b", 0), ("b", "b", 1), ("a", "a then c", 0), ("a", "a then c", 1)]:
            opened[name, piece] = bank(next_bank(role))
            t = piece // HALVES
            run_passes(opened[name, piece], piece, passes_a(t) if name == "a" else passes_b(t)[:1] + [None], 0, 1)
        ready = [refill(0)]
        for piece in range(PIECES):
            t, half = divmod(piece, HALVES)
            if piece + 1 < PIECES:
                ready.append(refill(piece + 1))
            if piece == 0:
                reorder_w3(1, nc.scalar.copy)
            scatter(piece, *ready[piece])
            if piece == PIECES - 2:
                gather_trucks(held("v2_w", [P, S2 // 2], I32))
        pairs = held("pairs", [P, 2, N, 2], BF16, "excess%d" % (PIECES - 1))
        for t in range(PACK - 1):
            for c in range(CHUNKS):
                round_chunk(t, c)
        gather_trucks(laid.tile([P, S2 // 2], I32, name="v2_w_last", offset=4 * T2 - S2, align_bytes=64))

        page_c = [held("page_c%d" % c, [P, N], I32) for c in range(CHUNKS)]
        page_s = [held("page_s%d" % c, [P, N], U8) for c in range(CHUNKS)]

        def quantize(c):
            words = page_rounded[c][:].rearrange("p n t -> p (n t)")
            nc.vector.quantize_mx(page_c[c][:].bitcast(FP8X4), page_s[c][:], words)

        for c in (2, 3, 0, 1):
            round_chunk(PACK - 1, c)
        quantize(0)
        nc.vector.tensor_copy(
            page_rounded[PAIR_CHUNK][:].rearrange("p n t -> p (n t)").bitcast(I32).rearrange("p (n u) -> p n u", u=2),
            pairs[:].rearrange("p u n e -> p (u n e)").bitcast(I32).rearrange("p (u n) -> p n u", u=2),
        )
        chunk_order = (0, 2, 1, 3)
        for c in chunk_order[1:]:
            quantize(c)

        e = [held("e%d" % n, [P, T2], F32) for n in range(GROUPS)]

        def score(n, c, number):
            acc_e = bank(number)
            nc.tensor.matmul_mx(
                acc_e[:], lhsT=v2_w[n // 2][:, span(n % 2, P)].bitcast(FP8X4), lhsT_scale=v2_s[:, span(n, P)],
                rhs=page_c[c][:].bitcast(FP8X4), rhs_scale=page_s[c][:], start=True, stop=True,
            )
            if (n, c) in VECTOR_COPIES:
                nc.vector.tensor_copy(e[n][:, span(c, N)], acc_e[:])
            else:
                nc.scalar.copy(e[n][:, span(c, N)], acc_e[:])

        for i, c in enumerate(chunk_order):
            for n in range(2):
                score(n, c, EARLY_BANKS[n][i])
        for i in range(2 * CHUNKS):
            score(2 + i // CHUNKS, chunk_order[i % CHUNKS], LATE_BANKS[i % len(LATE_BANKS)])
        picked = []
        for n in range(GROUPS):
            for first, count in (LAST_CUTS if n == GROUPS - 1 else CUTS):
                x = ring.tile([P, count], F32, name="x", tag="a_then_x")
                nc.vector.tensor_copy(x[:], e[n][:].indirect(list4[:, first // 16 : (first + count) // 16]))
                picked.append((n, slice(first, first + count), x))

        def square(x, engine):
            if engine is nc.scalar:
                nc.scalar.activation(x[:], x[:], ACT.Square)
            else:
                engine.tensor_tensor(x[:], x[:], x[:], ALU.mult)

        engines = {"S": nc.scalar, "V": nc.vector, "G": nc.gpsimd}
        for piece, (n, columns, x) in enumerate(picked):
            square(x, engines[FIRST_SQUARES[piece]])
            factor = inv_avail[:, n : n + 1]
            nc.scalar.activation(x[:], x[:], ACT.Abs_reciprocal_sqrt, bias=factor, scale=factor)
            square(x, engines[SECOND_SQUARES[piece]])
            nc.sync.dma_start(out[span(n, P), columns], x[:])
